import numpy as np, ml_dtypes
CORES = [16,18,20,22]
N = 4
import mx_ref
BF = ml_dtypes.bfloat16
def entries(a):
    return np.ascontiguousarray(a.T).reshape(-1)
def table(e):
    return np.ascontiguousarray(np.reshape(e, (-1, 16)).T).astype(np.int32)
def cut(t, i, w=512):
    return t[:, w * i:w * i + w]
def decode(q):
    o = []
    for b in range(4):
        e = np.zeros((128, 128, 4), np.float32); e[np.arange(128), np.arange(128), b] = 1
        o.append(mx_ref.matmul(mx_ref.quantize(e.reshape(128, 512).astype(BF)), q))
    return np.stack(o, axis=2).reshape(128, -1)
def f(rng, *shape):
    return mx_ref.flush((rng.standard_normal(shape, dtype=np.float32) * np.exp2(rng.integers(-2, 3, shape[:-1] + (1,)))).astype(BF))
def wide(rng, *shape, cols=0):
    v = rng.standard_normal(shape, dtype=np.float32) * np.exp2(rng.integers(-12, 13, shape)).astype(np.float32)
    if cols: v *= np.repeat(np.exp2(rng.integers(-cols, cols + 1, shape[:-2] + (1, shape[-1] // 4))) * (rng.random(shape[:-2] + (1, shape[-1] // 4)) > 0.0625), 4, axis=-1).astype(np.float32)
    return mx_ref.flush(v.astype(BF))
T, K, O = 512, 512, 2
HA = (1237, 1811, 947, 1543)
HB = (40503, 12289, 58111, 3571)
def setup_inputs(rng):
    return {"tb": f(rng, N, 128, 4 * K), "ids": np.stack([table(rng.integers(0, 4096, T)) for r in range(N)]), "w": f(rng, N, 128, 512 * O)}
def setup_inputs_alike(rng):
    d = setup_inputs(rng); e = rng.integers(0, 4096, T)
    d["ids"] = np.stack([table(e) for r in range(N)]); return d
def setup_inputs_ends(rng):
    d = setup_inputs(rng); o = []
    for r in range(N):
        e = rng.choice([0, 4095], T); e[rng.permutation(T)[:2]] = [0, 4095]
        o.append(table(e))
    d["ids"] = np.stack(o); return d
def setup_inputs_order(rng):
    d = setup_inputs(rng); t = rng.standard_normal((N, 128, 4 * K), dtype=np.float32)
    one = rng.permutation(np.concatenate([np.arange(N), rng.integers(0, N, 16 - N)]))
    for g in range(16):
        p = int(one[g]); o = int(rng.choice([q for q in range(N) if abs(q - p) >= 2]))
        size = np.float32(2.0 ** int(rng.integers(0, 3)))
        X = np.tile(rng.choice([-1, 1], (8, 4)).astype(np.float32) * size, (1, K))
        v = t[:, 8 * g:8 * g + 8]; v *= size * np.float32(2.0 ** -14)
        v[min(p, o)] = X; v[max(p, o)] = -X
    d["tb"] = mx_ref.flush(t.astype(BF)); return d
def setup_inputs_same(rng):
    d = setup_inputs(rng)
    d["ids"] = np.stack([table(np.full(T, rng.integers(0, 4096))) for r in range(N)]); return d
def setup_inputs_spread(rng):
    d = setup_inputs(rng); d["tb"] = wide(rng, N, 128, 4 * K, cols=8); return d
def check_inputs(d):
    b = []
    for r in range(N):
        e = entries(d["ids"][r])
        if e.min() < 0 or e.max() > 4095: b.append("ids")
    return b
def address(q, e):
    return ((e * HA[q] + HB[q]) >> 5) & (K - 1)
def reference(tb, ids, w):
    d = [decode(mx_ref.quantize(tb[q])).reshape(128, -1, 4) for q in range(N)]
    y = np.zeros((N, 128, O * T), np.float32)
    for r in range(N):
        e = entries(ids[r])
        v = d[0][:, address(0, e)]
        for q in range(1, N): v = v + d[q][:, address(q, e)]
        V = mx_ref.quantize(np.ascontiguousarray(v.reshape(128, -1)).astype(BF))
        for o in range(O): y[r][:, T * o:T * o + T] = mx_ref.matmul(mx_ref.quantize(np.ascontiguousarray(cut(w[r], o))), V)
    return {"y": y}

@@ -1,0 +1,252 @@
+from concourse.bass import DstId, RemoteDMATransfer
+from concourse.mybir import dt, AluOpType, ActivationFunctionType
+
+N, TOK, K, O = 4, 512, 512, 2
+HA = (1237, 1811, 947, 1543)
+HB = (40503, 12289, 58111, 3571)
+COPY = ActivationFunctionType.Copy
+CFG = {
+    "CUT": (320, 320, 288, 288),
+    "XOR": (2, 3, 1),
+    "NV": [[2, 2, 1], [2, 2, 2]],
+    "OV": [2, 1],
+    "SEQ": "00 01 02 03 t 10 11 w 12 13",
+    "PACK0": 0,
+    "LE": ((0, 8), (8, 12), (12, 16)),
+}
+
+SCRATCH = {
+    "ids8": ("sbuf", [128, 32], "int32"),
+    "hx": ("sbuf", [128, 128], "int32"),
+    "hh": ("sbuf", [128, 128], "int32"),
+    "mine": ("sbuf", [128, 256], "uint16"),
+    "mineo": ("sbuf", [128, 64], "uint16"),
+    "even": ("sbuf", [128, 192], "uint16"),
+    "odd": ("sbuf", [128, 192], "uint16"),
+    "tbt": ("sbuf", [128, 4 * K], "bfloat16"),
+    "wt": ("sbuf", [128, 512 * O], "bfloat16"),
+    "wq": ("sbuf", [128, 128 * O], "float8_e4m3fn_x4"),
+    "wp": ("sbuf", [128, 128 * O], "uint8"),
+    "one": ("sbuf", [128, 128], "bfloat16"),
+    "eye": ("sbuf", [128, 128], "bfloat16"),
+    "e": ("sbuf", [128, 528], "bfloat16"),
+    "eq": ("sbuf", [128, 512], "float8_e4m3fn_x4"),
+    "ep": ("sbuf", [128, 512], "uint8"),
+    "vt": ("sbuf", [128, 4 * TOK], "bfloat16"),
+    "vq": ("sbuf", [128, TOK], "float8_e4m3fn_x4"),
+    "vp": ("sbuf", [128, TOK], "uint8"),
+    "yt": ("sbuf", [128, O * TOK], "float32"),
+}
+for _s in range(4):
+    SCRATCH["gt%d" % _s] = ("sbuf", [128, 4 * TOK], "bfloat16")
+    SCRATCH["gq%d" % _s] = ("sbuf", [128, TOK], "float8_e4m3fn_x4")
+    SCRATCH["gp%d" % _s] = ("sbuf", [128, TOK], "uint8")
+for _s in range(1, 4):
+    SCRATCH["rq%d" % _s] = ("sbuf", [128, TOK], "float8_e4m3fn_x4")
+    SCRATCH["rp%d" % _s] = ("sbuf", [128, TOK], "uint8")
+for _b in range(8):
+    SCRATCH["ps%d" % _b] = ("psum", [128, 512], "float32")
+
+SEMAPHORES = ["sv", "ss", "sp", "sg", "li", "lt", "lw", "ly", "sent"] + \
+    ["la%d" % s for s in range(3)] + ["ar%d%d" % (s, c) for s in range(3) for c in range(2)]
+
+
+def rank_program(g, core, T, topo):
+    r = T.rank_of(core)
+    if r is None:
+        return
+    XOR = CFG["XOR"]
+    V, S, P, Y = g.vector, g.scalar, g.tensor, g.sync
+    Q = {"v": V, "s": S, "p": P, "g": g, "y": Y}
+    peer = [r ^ XOR[s] for s in range(3)]
+    pcore = [T.cores[p] for p in peer]
+    eng = [topo.engines(core, c) for c in pcore]
+    done, seen, local = {}, {}, [0]
+
+    def run(q, c):
+        return ((0, CFG["CUT"][q]), (CFG["CUT"][q], TOK))[c]
+
+    def fin(sem, ins, n=1):
+        ins.then_inc(T.sem[sem], n)
+        done[sem] = done.get(sem, 0) + n
+        return (sem, done[sem])
+
+    def need(q, *marks):
+        for sem, n in marks:
+            if seen.get((q, sem), 0) < n:
+                Q[q].wait_ge(T.sem[sem], n)
+                seen[(q, sem)] = n
+
+    def send(items):
+        tr = []
+        for s, es, src, dst, sem in items:
+            rid, pid, _ = topo.addr(pcore[s])
+            tr.append(RemoteDMATransfer(dst_ids=[DstId(rid=rid, pnc=pid)], dma_engine_mask=sum(1 << e for e in es),
+                                        remote_sem=T.sem[sem], srcs=[src], dsts=[dst]))
+            local[0] += len(es)
+        g.remote_dma_fused(tr, local_sem=T.sem.sent)
+
+    for i in range(4):
+        fin("li", Y.dma_start(T.ids8[16 * i:16 * i + 16, :], T.ids[:, :]), 16)
+        j = i + 4
+        m_ids = fin("li", S.dma_start(T.ids8[16 * j:16 * j + 16, :], T.ids[:, :]), 16)
+    m_tb = fin("lt", Y.dma_start(T.tbt[:], T.tb[:, :]), 16)
+    m_w = fin("lw", Y.dma_start(T.wt[:], T.w[:, :]), 16)
+
+    m_one = fin("sv", V.memset(T.one[:], 1.0))
+    need("g", m_one)
+    m_eye = fin("sg", g.affine_select(T.eye[:], T.one[:], [[-1, 128]], AluOpType.is_equal, 0.0, 0, 1))
+    need("v", fin("sv", V.memset(T.e[:], 0.0)), m_eye)
+    need("v", fin("sv", V.tensor_copy(T.e[:, 4:516:4], T.eye[:])))
+    for b in range(4):
+        m_e = fin("sv", V.quantize_mx(T.eq[:, 128 * b:128 * b + 128], T.ep[:, 128 * b:128 * b + 128], T.e[:, 4 - b:516 - b]))
+
+    tabs = peer + [r]
+
+    def columns(s0, s1):
+        for s in range(s0, s1):
+            m = fin("sv", V.tensor_scalar(T.hx[:, 32 * s:32 * s + 32], T.ids8[:], HA[tabs[s]], HB[tabs[s]], AluOpType.mult, AluOpType.add))
+        need("v", m)
+        need("v", fin("sv", V.tensor_scalar(T.hh[:, 32 * s0:32 * s1], T.hx[:, 32 * s0:32 * s1], 3, 4 * (K - 1),
+                                            AluOpType.logical_shift_right, AluOpType.bitwise_and)))
+
+    def evens(s):
+        h = T.hh[:, 32 * s:32 * s + 32]
+        fin("sv", V.tensor_copy(T.mine[:, 64 * s:64 * s + 32], h))
+        return fin("sv", V.tensor_scalar(T.mine[:, 64 * s + 32:64 * s + 64], h, 2, None, AluOpType.add))
+
+    def plus1(out, src, *marks):
+        need("v", *marks)
+        return fin("sv", V.tensor_scalar(out, src, 1, None, AluOpType.add))
+
+    def addresses(ss):
+        send([(s, eng[s][CFG["LE"][s][0]:CFG["LE"][s][1]], T.mine[:, 64 * s:64 * s + 64], T.even[:, 64 * s:64 * s + 64], "la%d" % s) for s in ss])
+
+    need("v", m_ids)
+    columns(0, 1)
+    need("g", evens(0))
+    addresses([0])
+    columns(1, 4)
+    m_ev = evens(3)
+    m_od = plus1(T.mineo[:], T.mine[:, 192:256], m_ev)
+    evens(1)
+    need("g", evens(2))
+    addresses([1, 2])
+    m_la = [("la%d" % s, z - a) for s, (a, z) in enumerate(CFG["LE"])]
+
+    m_off = {(0, 0): m_ev, (0, 1): m_od}
+    for s in range(3):
+        m_off[s + 1, 0] = m_la[s]
+
+    def gather(k, c, nv):
+        a, z = run(tabs[k - 1], c)
+        marks = []
+        for t in (0, 2, 1, 3):
+            if k == 0:
+                off, o = (T.mineo, 0) if t % 2 else (T.mine, 192)
+            else:
+                off, o = (T.odd if t % 2 else T.even), 64 * (k - 1)
+            o += 32 * (t // 2)
+            out = T["gt%d" % k][:, 4 * a + t:4 * z:4]
+            src = T.tbt[:].indirect(off[:, o + a // 16:o + z // 16])
+            q = "v" if t < nv else "s"
+            need(q, m_tb, m_off[k, t % 2])
+            if q == "v":
+                marks.append(fin("sv", V.tensor_copy(out, src)))
+            else:
+                marks.append(fin("ss", S.activation(out, src, COPY)))
+        return marks
+
+    def pack(k, c, marks):
+        a, z = run(tabs[k - 1], c)
+        need("v", *marks)
+        return fin("sv", V.quantize_mx(T["gq%d" % k][:, a:z], T["gp%d" % k][:, a:z], T["gt%d" % k][:, 4 * a:4 * z]))
+
+    m_own = {}
+    own0 = gather(0, 0, CFG["OV"][0])
+
+    arr = {}
+    for c in range(2):
+        for s in range(3):
+            k = s + 1
+            a, z = run(peer[s], c)
+            if c == 0 and s == CFG["PACK0"]:
+                m_own[0] = pack(0, 0, own0)
+            if c == 0 and s == 0:
+                m_off[1, 1] = plus1(T.odd[:, 0:64], T.even[:, 0:64], m_la[0])
+            marks = gather(k, c, CFG["NV"][c][s])
+            if c == 0 and s == 0:
+                m_off[2, 1] = m_off[3, 1] = plus1(T.odd[:, 64:192], T.even[:, 64:192], m_la[1], m_la[2])
+            need("g", pack(k, c, marks))
+            sem = "ar%d%d" % (s, c)
+            send([(s, eng[s], T["gq%d" % k][:, a:z].bitcast(dt.uint8), T["rq%d" % k][:, a:z].bitcast(dt.uint8), sem)])
+            send([(s, eng[s], T["gp%d" % k][:, a:z], T["rp%d" % k][:, a:z], sem)])
+            arr[peer[s], c] = (sem, 2 * len(eng[s]))
+    m_own[1] = pack(0, 1, gather(0, 1, CFG["OV"][1]))
+    need("v", m_w)
+    m_wq = fin("sv", V.quantize_mx(T.wq[:], T.wp[:], T.wt[:]))
+
+    order = [1, 0, 2, 3] if (r == 1 or r == 3) else [0, 1, 2, 3]
+    last, m_vq, my = {}, {}, {}
+
+    def decode(c, i):
+        (a, z), q, base = run(r, c), order[i], 4 * c
+        k = 0 if q == r else peer.index(q) + 1
+        cq, cp, mk = (T.gq0, T.gp0, m_own[c]) if q == r else (T["rq%d" % k], T["rp%d" % k], arr[q, c])
+        need("p", m_e, mk)
+        for b in range(4):
+            last[c, b] = fin("sp", P.matmul_mx(T["ps%d" % (base + b)][:, 0:z - a], T.eq[:, 128 * b:128 * b + 128],
+                                               T.ep[:, 128 * b:128 * b + 128], cq[:, a:z], cp[:, a:z], i == 0, i == 3))
+
+    def tile(c):
+        (a, z), base = run(r, c), 4 * c
+        mv = []
+        for b in range(4):
+            out, src = T.vt[:, 4 * a + b:4 * z:4], T["ps%d" % (base + b)][:, 0:z - a]
+            if b % 2 == 0:
+                need("v", last[c, b])
+                mv.append(fin("sv", V.tensor_copy(out, src)))
+            else:
+                need("s", last[c, b])
+                mv.append(fin("ss", S.activation(out, src, COPY)))
+        need("v", *mv)
+        m_vq[c] = fin("sv", V.quantize_mx(T.vq[:, a:z], T.vp[:, a:z], T.vt[:, 4 * a:4 * z]))
+
+    def product(c):
+        (a, z), base = run(r, c), 4 * c
+        need("p", m_wq, m_vq[c])
+        for o in range(O):
+            my[c, o] = fin("sp", P.matmul_mx(T["ps%d" % (base + o)][:, 0:z - a], T.wq[:, 128 * o:128 * o + 128],
+                                             T.wp[:, 128 * o:128 * o + 128], T.vq[:, a:z], T.vp[:, a:z], True, True))
+
+    def store(c):
+        (a, z), base = run(r, c), 4 * c
+        n = z - a
+        for o in range(O):
+            lo = TOK * o + a
+            out, src = T.yt[:, lo:lo + n], T["ps%d" % (base + o)][:, 0:n]
+            if o == 0:
+                need("v", my[c, o])
+                mk = fin("sv", V.tensor_copy(out, src))
+                dq = "y"
+            else:
+                need("s", my[c, o])
+                mk = fin("ss", S.activation(out, src, COPY))
+                dq = "s" if c == 1 else "y"
+            need(dq, mk)
+            fin("ly", Q[dq].dma_start(T.y[:, lo:lo + n], T.yt[:, lo:lo + n]), 16)
+
+    for op in CFG["SEQ"].split():
+        if op == "t":
+            tile(0)
+        elif op == "w":
+            product(0)
+            store(0)
+        else:
+            decode(int(op[0]), int(op[1]))
+    tile(1)
+    product(1)
+    store(1)
+    g.wait_ge(T.sem.sent, local[0])
+    for sem in ("sv", "ss", "sp", "sg", "ly"):
+        need("g", (sem, done[sem]))

@@ -5,33 +5,62 @@ N, TOK, K, O = 4, 512, 512, 2
 HA = (1237, 1811, 947, 1543)
 HB = (40503, 12289, 58111, 3571)
 COPY = ActivationFunctionType.Copy
+ADD = AluOpType.add
 CFG = {
-    "CUT": (320, 320, 288, 288),
-    "XOR": (2, 3, 1),
-    "NV": [[2, 2, 1], [2, 2, 2]],
-    "OV": [2, 1],
-    "SEQ": "00 01 02 03 t 10 11 w 12 13",
-    "PACK0": 0,
-    "LE": ((0, 8), (8, 12), (12, 16)),
+    "CUT": (256, 256, 192, 192),
+    "WLOAD": 1,
+    "PICK": [[("h0", 1, ""), ("h1", 2, "h0+h1"), ("r2", 2, "r2"), ("r3", 1, "r3"), ("r1", 2, "r1"), ("r0", 1, "")]] * 2,
+    "ORDER": ((0, 1, 2, 3), (1, 0, 2, 3), (0, 1, 2, 3), (1, 0, 2, 3)),
+    "PE": ("0123 r h", "0123 r h", "0 1 23 r h", "0 1 23 r h"),
+    "STEP": 1,
+    "HSTEP": 2,
+    "ESEND": 1,
+    "AE": ((0, 4), (4, 6), (6, 8), (8, 10)),
+    "FIRST": ("mwfh", "mwa"),
+    "LATE": ((0, 2, 3), (0, 2, 3)),
+    "WHOLE": "q01 p01",
+    "RUNS": ((), ()),
+    "HP": ("a0 a1 a2 a3 b0 b1 b2 b3 p0 p1 p2 p3", "a0 a1 a2 a3 b0 b1 b2 b3 p0 q0 p1 q1 p2 q2 p3 q3"),
+    "HV": ("a0 a2 b0 b1 x0 z0 x1 z1 x2 z2 x3 z3 s0", "a0 a2 b0 b1 x0 y0 z0 x1 y1 z1 x2 y2 z2 x3 y3 z3 s0"),
+    "HS": ("a1 a3 g0 g1 g2 b2 g3 b3", "a1 a3 g0 g1 b2 g2 b3 g3"),
 }
+CFG.update({'CUT': (256, 256, 224, 224),
+ 'PICK': [[('h0', 1, ''), ('h1', 2, 'h0+h1'), ('r1', 1.5, 'r1'), ('r2', 1.5, 'r2'), ('r3', 2.0, 'r3'), ('r0', 1.5, '')],
+          [('h0', 1.5, ''), ('h1', 2.0, 'h0+h1'), ('r0', 1.5, ''), ('r1', 2.0, 'r1'), ('r2', 1.5, 'r2'), ('r3', 1.5, 'r3')]],
+ 'ORDER': ((1, 0, 2, 3), (0, 1, 2, 3), (0, 1, 2, 3), (1, 0, 2, 3)), 'RUNS': ((), ()),
+ 'PE': ('0 1 23 r h', '0 1 23 r h', '0 1 2 3 r h', '0 1 2 3 r h'),
+ 'HV': ('a0 a2 b0 b2 x0 x1 z0 x2 z1 x3 z2 z3 s0', 'a0 a2 b0 b1 x0 x1 y0 x2 y1 z0 x3 y2 z1 y3 z2 z3 s0'),
+ 'HS': ('a1 a3 g0 b1 g1 g2 b3 g3', 'a1 a3 g0 g1 b2 g2 b3 g3'),
+ 'WLOAD': 2,
+ 'WHOLE': 'q01 p01',
+ 'LATE': ((0, 2, 3, 4), (0, 2, 3)),
+ 'FIRST': ('mwfh', 'mwa')})
 
 SCRATCH = {
     "ids8": ("sbuf", [128, 32], "int32"),
     "hx": ("sbuf", [128, 128], "int32"),
-    "hh": ("sbuf", [128, 128], "int32"),
-    "mine": ("sbuf", [128, 256], "uint16"),
-    "mineo": ("sbuf", [128, 64], "uint16"),
-    "even": ("sbuf", [128, 192], "uint16"),
-    "odd": ("sbuf", [128, 192], "uint16"),
+    "hh": ("sbuf", [128, 4, 32], "int32"),
+    "near": ("sbuf", [128, 2, 64], "uint16"),
+    "nearo": ("sbuf", [128, 64], "uint16"),
+    "far": ("sbuf", [128, 2, 64], "uint16"),
+    "hlp": ("sbuf", [128, 64], "uint16"),
+    "even": ("sbuf", [128, 3, 64], "uint16"),
+    "odd": ("sbuf", [128, 3, 64], "uint16"),
+    "hoff": ("sbuf", [128, 64], "uint16"),
     "tbt": ("sbuf", [128, 4 * K], "bfloat16"),
+    "tq": ("sbuf", [128, K], "float8_e4m3fn_x4"),
+    "tp": ("sbuf", [128, K], "uint8"),
     "wt": ("sbuf", [128, 512 * O], "bfloat16"),
     "wq": ("sbuf", [128, 128 * O], "float8_e4m3fn_x4"),
     "wp": ("sbuf", [128, 128 * O], "uint8"),
-    "one": ("sbuf", [128, 128], "bfloat16"),
     "eye": ("sbuf", [128, 128], "bfloat16"),
     "e": ("sbuf", [128, 528], "bfloat16"),
     "eq": ("sbuf", [128, 512], "float8_e4m3fn_x4"),
     "ep": ("sbuf", [128, 512], "uint8"),
+    "da": ("sbuf", [128, 4 * K], "bfloat16"),
+    "db": ("sbuf", [128, 4 * K], "bfloat16"),
+    "ga": ("sbuf", [128, 4 * TOK], "bfloat16"),
+    "acc": ("sbuf", [128, 4 * TOK], "float32"),
     "vt": ("sbuf", [128, 4 * TOK], "bfloat16"),
     "vq": ("sbuf", [128, TOK], "float8_e4m3fn_x4"),
     "vp": ("sbuf", [128, TOK], "uint8"),
@@ -41,30 +70,24 @@ for _s in range(4):
     SCRATCH["gt%d" % _s] = ("sbuf", [128, 4 * TOK], "bfloat16")
     SCRATCH["gq%d" % _s] = ("sbuf", [128, TOK], "float8_e4m3fn_x4")
     SCRATCH["gp%d" % _s] = ("sbuf", [128, TOK], "uint8")
-for _s in range(1, 4):
     SCRATCH["rq%d" % _s] = ("sbuf", [128, TOK], "float8_e4m3fn_x4")
     SCRATCH["rp%d" % _s] = ("sbuf", [128, TOK], "uint8")
 for _b in range(8):
     SCRATCH["ps%d" % _b] = ("psum", [128, 512], "float32")
 
-SEMAPHORES = ["sv", "ss", "sp", "sg", "li", "lt", "lw", "ly", "sent"] + \
-    ["la%d" % s for s in range(3)] + ["ar%d%d" % (s, c) for s in range(3) for c in range(2)]
+SEMAPHORES = ["sv", "ss", "sp", "sg", "li", "lt", "lw", "ly", "sent", "lh", "av0", "av1", "ae"] + \
+    ["la%d" % x for x in range(1, 4)] + ["ar%d" % x for x in range(4)]
 
 
 def rank_program(g, core, T, topo):
-    r = T.rank_of(core)
-    if r is None:
+    spare = [c for c in topo.cores_of(T.cores[0]) if c not in T.cores]
+    helper = [[c for c in spare if topo.die(c) == topo.die(T.cores[q ^ 2])][q % 2] for q in range(N)]
+    if core not in T.cores and core not in helper:
         return
-    XOR = CFG["XOR"]
     V, S, P, Y = g.vector, g.scalar, g.tensor, g.sync
     Q = {"v": V, "s": S, "p": P, "g": g, "y": Y}
-    peer = [r ^ XOR[s] for s in range(3)]
-    pcore = [T.cores[p] for p in peer]
-    eng = [topo.engines(core, c) for c in pcore]
+    CUT = CFG["CUT"]
     done, seen, local = {}, {}, [0]
-
-    def run(q, c):
-        return ((0, CFG["CUT"][q]), (CFG["CUT"][q], TOK))[c]
 
     def fin(sem, ins, n=1):
         ins.then_inc(T.sem[sem], n)
@@ -77,176 +100,313 @@ def rank_program(g, core, T, topo):
                 Q[q].wait_ge(T.sem[sem], n)
                 seen[(q, sem)] = n
 
-    def send(items):
+    def share(src, dst, i, n, step=None):
+        es = topo.engines(src, dst)[::step or CFG["STEP"]]
+        e = len(es)
+        cut = {1: (0, e), 2: (0, e // 2, e), 3: (0, e // 4, e // 2, e)}[n]
+        return es[cut[i]:cut[i + 1]]
+
+    def send(items, es=None, step=None):
         tr = []
-        for s, es, src, dst, sem in items:
-            rid, pid, _ = topo.addr(pcore[s])
-            tr.append(RemoteDMATransfer(dst_ids=[DstId(rid=rid, pnc=pid)], dma_engine_mask=sum(1 << e for e in es),
-                                        remote_sem=T.sem[sem], srcs=[src], dsts=[dst]))
-            local[0] += len(es)
+        for i, (dst_core, src, dst, sem) in enumerate(items):
+            cores = dst_core if isinstance(dst_core, list) else [dst_core]
+            e = es[i] if es else share(core, cores[0], i, len(items), step)
+            tr.append(RemoteDMATransfer(dst_ids=[DstId(rid=topo.addr(c)[0], pnc=topo.addr(c)[1]) for c in cores],
+                                        dma_engine_mask=sum(1 << k for k in e), remote_sem=T.sem[sem], srcs=[src], dsts=[dst] * len(cores)))
+            local[0] += len(e)
         g.remote_dma_fused(tr, local_sem=T.sem.sent)
+
+    def u8(buf, a, z):
+        return buf[:, a:z].bitcast(dt.uint8)
+
+    def constants():
+        m_eye = fin("sg", g.iota(T.eye[:], [[-1, 128]], 0, 1, allow_small_or_imprecise_dtypes=True))
+        need("v", fin("sv", V.memset(T.e[:], 0.0)), m_eye)
+        need("v", fin("sv", V.tensor_scalar(T.e[:, 4:516:4], T.eye[:], 0.0, None, AluOpType.is_equal)))
+        for b in range(4):
+            m = fin("sv", V.quantize_mx(T.eq[:, 128 * b:128 * b + 128], T.ep[:, 128 * b:128 * b + 128], T.e[:, 4 - b:516 - b]))
+        return m
+
+    def runs(q):
+        cuts = (0,) + CFG["RUNS"][q // 2] + (CUT[q],)
+        return list(zip(cuts, cuts[1:]))
+
+    def decode(base, cq, cp, a, z, start, stop, banks):
+        ms = []
+        for b in banks:
+            ms.append(fin("sp", P.matmul_mx(T["ps%d" % (base + b)][:, 0:z - a], T.eq[:, 128 * b:128 * b + 128],
+                                            T.ep[:, 128 * b:128 * b + 128], cq[:, a:z], cp[:, a:z], start, stop)))
+        return ms
+
+    def copy(q, out, src):
+        return fin("sv", V.tensor_copy(out, src)) if q == "v" else fin("ss", S.activation(out, src, COPY))
+
+    def whole_engines(q, h):
+        n = 0
+        for call in CFG["WHOLE"].split():
+            i = str((h ^ q) % 2)
+            if len(call) == 1:
+                n += len(share(T.cores[q], helper[h], 0, 1))
+            elif i in call:
+                n += len(share(T.cores[q], helper[h], call.index(i) - 1, len(call) - 1))
+        return n
+
+    def landed(q, name):
+        for _, _, calls in CFG["PICK"][q // 2]:
+            for call in calls.split():
+                parts = call.split("+")
+                if name in parts:
+                    return ("ar" + name[1], 2 * len(share(T.cores[q], core, parts.index(name), len(parts))))
+
+    def addr_engines(q):
+        es = topo.engines(T.cores[q], T.cores[q ^ 1])[::CFG["STEP"]]
+        return [es[a:z] for a, z in CFG["AE"]]
+
+    if core in helper:
+        r = helper.index(core)
+        n, kind = CUT[r], r // 2
+        k = n // 16
+        m_e = constants()
+        if CFG["ESEND"]:
+            need("g", m_e)
+            send([(T.cores[r], u8(T.eq, 0, 512), u8(T.eq, 0, 512), "ae")], step=CFG["HSTEP"])
+            send([(T.cores[r], T.ep[:], T.ep[:], "ae")], step=CFG["HSTEP"])
+        xa, xb = ((2 ^ r, 3 ^ r), (0 ^ r, 1 ^ r))[kind]
+        xp, xq = ((0, 1), (2 ^ r, 3 ^ r))[kind]
+        m_off = ("lh", len(addr_engines(r)[3]))
+        m_pick = {x: landed(r ^ x, "h%d" % x) for x in (0, 1)}
+        mk = {}
+        todo = {"p": CFG["HP"][kind].split(), "v": CFG["HV"][kind].split(), "s": CFG["HS"][kind].split()}
+
+        def step(q, op):
+            c, b = op[0], int(op[1])
+            if q == "p":
+                if c in "ab":
+                    x = 2 + (c == "b")
+                    need("p", m_e, ("ar%d" % x, whole_engines(r ^ (xa if c == "a" else xb), r)))
+                    mk["d" + c, b] = decode(4 * (c == "b"), T["rq%d" % x], T["rp%d" % x], 0, K, True, True, (b,))[0]
+                else:
+                    free = ("a" if c == "p" else "b", b)
+                    if free not in mk:
+                        return False
+                    xs = (xp, xq) if kind == 0 else (xp if c == "p" else xq,)
+                    for x in xs:
+                        need("p", mk[free], m_pick[x])
+                        mk["d" + c, b] = decode(4 * (c == "q"), T["rq%d" % x], T["rp%d" % x], 0, n, x == xs[0], x == xs[-1], (b,))[0]
+            elif c in "ab":
+                if ("d" + c, b) not in mk:
+                    return False
+                need(q, mk["d" + c, b])
+                mk[c, b] = copy(q, T["d" + c][:, K * b:K * b + K], T["ps%d" % (4 * (c == "b") + b)][:])
+            elif c == "g":
+                if ("a", b) not in mk:
+                    return False
+                need(q, mk["a", b], m_off)
+                mk[c, b] = copy(q, T.ga[:, n * b:n * b + n], T.da[:, K * b:K * b + K].indirect(T.hoff[:, (xa - 2) * k:(xa - 1) * k]))
+            elif c == "s":
+                lo, hi = runs(r)[b]
+                need("v", *[mk["z", i] for i in range(4)])
+                need("g", fin("sv", V.quantize_mx(T.vq[:, lo:hi], T.vp[:, lo:hi], T.vt[:, 4 * lo:4 * hi])))
+                send([(T.cores[r], u8(T.vq, lo, hi), u8(T.vq, lo, hi), "av%d" % b)], step=CFG["HSTEP"])
+                send([(T.cores[r], T.vp[:, lo:hi], T.vp[:, lo:hi], "av%d" % b)], step=CFG["HSTEP"])
+            else:
+                lo, hi = runs(r)[int(op[2])] if op[2:] else (0, n)
+                before = {"x": "g", "y": "x", "z": "xy"[kind]}[c]
+                picked = (c == "z") if kind == 0 else (c == "x")
+                src = ("b" if picked else "dq" if c == "z" else "dp", b)
+                if (before, b) not in mk or src not in mk:
+                    return False
+                acc = T.acc[:, n * b + lo:n * b + hi]
+                old = T.ga[:, n * b + lo:n * b + hi] if c == "x" else acc
+                need("v", mk[src], mk[before, b])
+                if picked:
+                    need("v", m_off)
+                    new = T.db[:, K * b:K * b + K].indirect(T.hoff[:, (xb - 2) * k + lo // 16:(xb - 2) * k + hi // 16])
+                else:
+                    new = T["ps%d" % (4 * (src[0] == "dq") + b)][:, lo:hi]
+                mk[c, b] = fin("sv", V.tensor_tensor(T.vt[:, 4 * lo + b:4 * hi:4] if c == "z" else acc, new, old, ADD))
+            return True
+
+        while any(todo.values()):
+            for q in "pvs":
+                while todo[q] and step(q, todo[q][0]):
+                    todo[q].pop(0)
+        g.wait_ge(T.sem.sent, local[0])
+        for sem in ("sv", "ss", "sp", "sg"):
+            need("g", (sem, done[sem]))
+        return
+
+    r = T.rank_of(core)
+    n = CUT[r]
+    k, kr = n // 16, (TOK - n) // 16
 
     for i in range(4):
         fin("li", Y.dma_start(T.ids8[16 * i:16 * i + 16, :], T.ids[:, :]), 16)
         j = i + 4
         m_ids = fin("li", S.dma_start(T.ids8[16 * j:16 * j + 16, :], T.ids[:, :]), 16)
     m_tb = fin("lt", Y.dma_start(T.tbt[:], T.tb[:, :]), 16)
-    m_w = fin("lw", Y.dma_start(T.wt[:], T.w[:, :]), 16)
+    m_e = ("ae", 2 * len(share(helper[r], core, 0, 1, CFG["HSTEP"]))) if CFG["ESEND"] else constants()
 
-    m_one = fin("sv", V.memset(T.one[:], 1.0))
-    need("g", m_one)
-    m_eye = fin("sg", g.affine_select(T.eye[:], T.one[:], [[-1, 128]], AluOpType.is_equal, 0.0, 0, 1))
-    need("v", fin("sv", V.memset(T.e[:], 0.0)), m_eye)
-    need("v", fin("sv", V.tensor_copy(T.e[:, 4:516:4], T.eye[:])))
-    for b in range(4):
-        m_e = fin("sv", V.quantize_mx(T.eq[:, 128 * b:128 * b + 128], T.ep[:, 128 * b:128 * b + 128], T.e[:, 4 - b:516 - b]))
-
-    tabs = peer + [r]
-
-    def columns(s0, s1):
-        for s in range(s0, s1):
-            m = fin("sv", V.tensor_scalar(T.hx[:, 32 * s:32 * s + 32], T.ids8[:], HA[tabs[s]], HB[tabs[s]], AluOpType.mult, AluOpType.add))
-        need("v", m)
-        need("v", fin("sv", V.tensor_scalar(T.hh[:, 32 * s0:32 * s1], T.hx[:, 32 * s0:32 * s1], 3, 4 * (K - 1),
-                                            AluOpType.logical_shift_right, AluOpType.bitwise_and)))
-
-    def evens(s):
-        h = T.hh[:, 32 * s:32 * s + 32]
-        fin("sv", V.tensor_copy(T.mine[:, 64 * s:64 * s + 32], h))
-        return fin("sv", V.tensor_scalar(T.mine[:, 64 * s + 32:64 * s + 64], h, 2, None, AluOpType.add))
+    tabs = [r ^ 1, r, r ^ 2, r ^ 3]
 
     def plus1(out, src, *marks):
         need("v", *marks)
-        return fin("sv", V.tensor_scalar(out, src, 1, None, AluOpType.add))
+        return fin("sv", V.tensor_scalar(out, src, 1, None, ADD))
 
-    def addresses(ss):
-        send([(s, eng[s][CFG["LE"][s][0]:CFG["LE"][s][1]], T.mine[:, 64 * s:64 * s + 64], T.even[:, 64 * s:64 * s + 64], "la%d" % s) for s in ss])
-
+    ae = addr_engines(r)
     need("v", m_ids)
-    columns(0, 1)
-    need("g", evens(0))
-    addresses([0])
-    columns(1, 4)
-    m_ev = evens(3)
-    m_od = plus1(T.mineo[:], T.mine[:, 192:256], m_ev)
-    evens(1)
-    need("g", evens(2))
-    addresses([1, 2])
-    m_la = [("la%d" % s, z - a) for s, (a, z) in enumerate(CFG["LE"])]
+    m_hx = [fin("sv", V.tensor_scalar(T.hx[:, 32 * s:32 * s + 32], T.ids8[:], HA[tabs[s]], HB[tabs[s]], AluOpType.mult, ADD)) for s in range(4)]
+    m_hh = []
+    for s in (0, 2):
+        need("v", m_hx[s + 1])
+        m_hh.append(fin("sv", V.tensor_scalar(T.hh[:, s:s + 2, :], T.hx[:, 32 * s:32 * s + 64], 3, 4 * (K - 1),
+                                              AluOpType.logical_shift_right, AluOpType.bitwise_and)))
+    need("v", m_hh[0])
+    fin("sv", V.tensor_copy(T.near[:, :, 0:32], T.hh[:, 0:2, :]))
+    m_ev = fin("sv", V.tensor_scalar(T.near[:, :, 32:64], T.hh[:, 0:2, :], 2, None, ADD))
+    need("v", m_hh[1])
+    fin("sv", V.tensor_copy(T.far[:, :, 0:kr], T.hh[:, 2:4, k:32]))
+    m_od = plus1(T.nearo[:], T.near[:, 1, :], m_ev)
+    fin("sv", V.tensor_scalar(T.far[:, :, kr:2 * kr], T.hh[:, 2:4, k:32], 2, None, ADD))
+    m_far = fin("sv", V.tensor_scalar(T.hlp[:, 0:2 * k], T.hh[:, 2:4, 0:k], 0.25, None, AluOpType.mult))
+    m_la = {x: ("la%d" % x, len(ae[x - 1])) for x in (1, 2, 3)}
+    need("v", m_tb)
+    m_tq = fin("sv", V.quantize_mx(T.tq[:], T.tp[:], T.tbt[:]))
+
+    def first_calls(op):
+        if op == "m":
+            need("g", m_ev)
+            send([(T.cores[r ^ 1], T.near[:, 0, :], T.even[:, 0, :], "la1")], ae[0:1])
+        elif op == "w":
+            need("g", m_tq)
+            x = 2 + r % 2
+            for call in CFG["WHOLE"].split():
+                src, dst = (u8(T.tq, 0, K), u8(T["rq%d" % x], 0, K)) if call[0] == "q" else (T.tp[:], T["rp%d" % x][:])
+                if len(call) == 1:
+                    send([([helper[r ^ 2], helper[r ^ 3]], src, dst, "ar%d" % x)])
+                else:
+                    send([(helper[r ^ (2 + int(i))], src, dst, "ar%d" % x) for i in call[1:]])
+        else:
+            need("g", m_far)
+            items = [(T.cores[r ^ x], T.far[:, x - 2, 0:2 * kr], T.even[:, x - 1, 0:2 * kr], "la%d" % x) for x in (2, 3)]
+            items.append((helper[r], T.hlp[:, 0:2 * k], T.hoff[:, 0:2 * k], "lh"))
+            if op == "a":
+                send(items, ae[1:])
+            elif op == "f":
+                send(items[0:2], ae[1:3])
+            else:
+                send(items[2:], ae[3:])
+
+    for op in CFG["FIRST"][k == kr]:
+        first_calls(op)
 
     m_off = {(0, 0): m_ev, (0, 1): m_od}
-    for s in range(3):
-        m_off[s + 1, 0] = m_la[s]
+    for x in (1, 2, 3):
+        m_off[x, 0] = m_la[x]
 
-    def gather(k, c, nv):
-        a, z = run(tabs[k - 1], c)
+    def gather(x, a, z, nv):
         marks = []
         for t in (0, 2, 1, 3):
-            if k == 0:
-                off, o = (T.mineo, 0) if t % 2 else (T.mine, 192)
-            else:
-                off, o = (T.odd if t % 2 else T.even), 64 * (k - 1)
-            o += 32 * (t // 2)
-            out = T["gt%d" % k][:, 4 * a + t:4 * z:4]
-            src = T.tbt[:].indirect(off[:, o + a // 16:o + z // 16])
-            q = "v" if t < nv else "s"
-            need(q, m_tb, m_off[k, t % 2])
-            if q == "v":
-                marks.append(fin("sv", V.tensor_copy(out, src)))
-            else:
-                marks.append(fin("ss", S.activation(out, src, COPY)))
+            first = 32 * (t // 2) if x < 2 else (z - a) // 16 * (t // 2) - a // 16
+            mid = a + round(min(1, max(0, nv - t)) * (z - a) / 32) * 32
+            for q, lo, hi in (("v", a, mid), ("s", mid, z)):
+                if lo == hi:
+                    continue
+                cols = slice(first + lo // 16, first + hi // 16)
+                if x == 0:
+                    off = T.nearo[:, cols] if t % 2 else T.near[:, 1, cols]
+                else:
+                    off = (T.odd if t % 2 else T.even)[:, x - 1, cols]
+                need(q, m_tb, m_off[x, t % 2])
+                marks.append(copy(q, T["gt%d" % x][:, 4 * lo + t:4 * hi:4], T.tbt[:].indirect(off)))
+                if q == "v" and late:
+                    late.pop()()
+        if late:
+            late.pop()()
         return marks
 
-    def pack(k, c, marks):
-        a, z = run(tabs[k - 1], c)
+    def pack(x, a, z, marks):
         need("v", *marks)
-        return fin("sv", V.quantize_mx(T["gq%d" % k][:, a:z], T["gp%d" % k][:, a:z], T["gt%d" % k][:, 4 * a:4 * z]))
+        return fin("sv", V.quantize_mx(T["gq%d" % x][:, a:z], T["gp%d" % x][:, a:z], T["gt%d" % x][:, 4 * a:4 * z]))
 
-    m_own = {}
-    own0 = gather(0, 0, CFG["OV"][0])
+    def part(name):
+        x = int(name[1])
+        return (x,) + {"h": (0, CUT[r ^ x]), "r": (CUT[r ^ x], TOK), "a": (0, TOK)}[name[0]]
 
-    arr = {}
-    for c in range(2):
-        for s in range(3):
-            k = s + 1
-            a, z = run(peer[s], c)
-            if c == 0 and s == CFG["PACK0"]:
-                m_own[0] = pack(0, 0, own0)
-            if c == 0 and s == 0:
-                m_off[1, 1] = plus1(T.odd[:, 0:64], T.even[:, 0:64], m_la[0])
-            marks = gather(k, c, CFG["NV"][c][s])
-            if c == 0 and s == 0:
-                m_off[2, 1] = m_off[3, 1] = plus1(T.odd[:, 64:192], T.even[:, 64:192], m_la[1], m_la[2])
-            need("g", pack(k, c, marks))
-            sem = "ar%d%d" % (s, c)
-            send([(s, eng[s], T["gq%d" % k][:, a:z].bitcast(dt.uint8), T["rq%d" % k][:, a:z].bitcast(dt.uint8), sem)])
-            send([(s, eng[s], T["gp%d" % k][:, a:z], T["rp%d" % k][:, a:z], sem)])
-            arr[peer[s], c] = (sem, 2 * len(eng[s]))
-    m_own[1] = pack(0, 1, gather(0, 1, CFG["OV"][1]))
-    need("v", m_w)
-    m_wq = fin("sv", V.quantize_mx(T.wq[:], T.wp[:], T.wt[:]))
+    stages = CFG["PICK"][r // 2]
+    late, mk = [], {}
 
-    order = [1, 0, 2, 3] if (r == 1 or r == 3) else [0, 1, 2, 3]
-    last, m_vq, my = {}, {}, {}
+    def pack_w():
+        need("v", mk["w"])
+        mk["wq"] = fin("sv", V.quantize_mx(T.wq[:], T.wp[:], T.wt[:]))
 
-    def decode(c, i):
-        (a, z), q, base = run(r, c), order[i], 4 * c
-        k = 0 if q == r else peer.index(q) + 1
-        cq, cp, mk = (T.gq0, T.gp0, m_own[c]) if q == r else (T["rq%d" % k], T["rp%d" % k], arr[q, c])
-        need("p", m_e, mk)
-        for b in range(4):
-            last[c, b] = fin("sp", P.matmul_mx(T["ps%d" % (base + b)][:, 0:z - a], T.eq[:, 128 * b:128 * b + 128],
-                                               T.ep[:, 128 * b:128 * b + 128], cq[:, a:z], cp[:, a:z], i == 0, i == 3))
+    def close(i, marks):
+        name, _, calls = stages[i]
+        x, a, z = part(name)
+        m = pack(x, a, z, marks)
+        if i == CFG["WLOAD"]:
+            need("y", m)
+            mk["w"] = fin("lw", Y.dma_start(T.wt[:], T.w[:, :]), 16)
+        if x == 0 and z == TOK:
+            mk["own"] = m
+        for call in calls.split():
+            need("g", m)
+            parts = [((helper if u[0] == "h" else T.cores)[r ^ int(u[1])],) + part(u) for u in call.split("+")]
+            send([(c, u8(T["gq%d" % x], a, z), u8(T["rq%d" % x], a, z), "ar%d" % x) for c, x, a, z in parts])
+            send([(c, T["gp%d" % x][:, a:z], T["rp%d" % x][:, a:z], "ar%d" % x) for c, x, a, z in parts])
 
-    def tile(c):
-        (a, z), base = run(r, c), 4 * c
-        mv = []
-        for b in range(4):
-            out, src = T.vt[:, 4 * a + b:4 * z:4], T["ps%d" % (base + b)][:, 0:z - a]
-            if b % 2 == 0:
-                need("v", last[c, b])
-                mv.append(fin("sv", V.tensor_copy(out, src)))
-            else:
-                need("s", last[c, b])
-                mv.append(fin("ss", S.activation(out, src, COPY)))
-        need("v", *mv)
-        m_vq[c] = fin("sv", V.quantize_mx(T.vq[:, a:z], T.vp[:, a:z], T.vt[:, 4 * a:4 * z]))
+    for i, (name, nv, calls) in enumerate(stages):
+        x, a, z = part(name)
+        if x == 1 and (x, 1) not in m_off:
+            m_off[x, 1] = plus1(T.odd[:, 0, :], T.even[:, 0, :], m_la[1])
+        if x > 1 and (x, 1) not in m_off:
+            w2 = (TOK - CUT[r ^ 2]) // 8
+            m_off[2, 1] = m_off[3, 1] = plus1(T.odd[:, 1:3, 0:w2], T.even[:, 1:3, 0:w2], m_la[2], m_la[3])
+        marks = gather(x, a, z, nv)
+        if i == len(stages) - 1 and not calls:
+            pack_w()
+        if i in CFG["LATE"][r // 2]:
+            late.append(lambda i=i, marks=marks: close(i, marks))
+        else:
+            close(i, marks)
+    if calls:
+        pack_w()
+    m_own, m_wq = mk["own"], mk["wq"]
 
-    def product(c):
-        (a, z), base = run(r, c), 4 * c
-        need("p", m_wq, m_vq[c])
-        for o in range(O):
-            my[c, o] = fin("sp", P.matmul_mx(T["ps%d" % (base + o)][:, 0:z - a], T.wq[:, 128 * o:128 * o + 128],
-                                             T.wp[:, 128 * o:128 * o + 128], T.vq[:, a:z], T.vp[:, a:z], True, True))
-
-    def store(c):
-        (a, z), base = run(r, c), 4 * c
-        n = z - a
+    order = CFG["ORDER"][r]
+    m_vq = {"hi"[i]: ("av%d" % i, 2 * len(share(helper[r], core, 0, 1, CFG["HSTEP"]))) for i in range(2)}
+    ops = CFG["PE"][r].split()
+    for op in ops:
+        if op.isdigit():
+            sums = []
+            for b in range(4):
+                for i in map(int, op):
+                    x = order[i] ^ r
+                    cq, cp, m = (T["rq%d" % x], T["rp%d" % x], landed(r ^ x, "r%d" % x)) if x else (T.gq0, T.gp0, m_own)
+                    need("p", m_e, m)
+                    m = decode(0, cq, cp, n, TOK, i == 0, i == 3, banks=(b,))
+                sums += m
+            if i == 3:
+                mv = []
+                for b in range(4):
+                    need("vs"[b % 2], sums[b])
+                    mv.append(copy("vs"[b % 2], T.vt[:, 4 * n + b:4 * TOK:4], T["ps%d" % b][:, 0:TOK - n]))
+                need("v", *mv)
+                m_vq["r"] = fin("sv", V.quantize_mx(T.vq[:, n:TOK], T.vp[:, n:TOK], T.vt[:, 4 * n:4 * TOK]))
+            continue
+        (a, z), base = ((n, TOK), 4) if op == "r" else (runs(r)[0], 6) if op == "h" else (runs(r)[1], 0)
+        need("p", m_wq, m_vq[op])
+        if op == "i":
+            need("p", *mv)
+        my = [fin("sp", P.matmul_mx(T["ps%d" % (base + o)][:, 0:z - a], T.wq[:, 128 * o:128 * o + 128], T.wp[:, 128 * o:128 * o + 128],
+                                    T.vq[:, a:z], T.vp[:, a:z], True, True)) for o in range(O)]
         for o in range(O):
             lo = TOK * o + a
-            out, src = T.yt[:, lo:lo + n], T["ps%d" % (base + o)][:, 0:n]
-            if o == 0:
-                need("v", my[c, o])
-                mk = fin("sv", V.tensor_copy(out, src))
-                dq = "y"
-            else:
-                need("s", my[c, o])
-                mk = fin("ss", S.activation(out, src, COPY))
-                dq = "s" if c == 1 else "y"
-            need(dq, mk)
-            fin("ly", Q[dq].dma_start(T.y[:, lo:lo + n], T.yt[:, lo:lo + n]), 16)
-
-    for op in CFG["SEQ"].split():
-        if op == "t":
-            tile(0)
-        elif op == "w":
-            product(0)
-            store(0)
-        else:
-            decode(int(op[0]), int(op[1]))
-    tile(1)
-    product(1)
-    store(1)
+            need("vs"[o], my[o])
+            m = copy("vs"[o], T.yt[:, lo:lo + z - a], T["ps%d" % (base + o)][:, 0:z - a])
+            dq = "s" if o == 1 and op == ops[-1] else "y"
+            need(dq, m)
+            fin("ly", Q[dq].dma_start(T.y[:, lo:lo + z - a], T.yt[:, lo:lo + z - a]), 16)
     g.wait_ge(T.sem.sent, local[0])
-    for sem in ("sv", "ss", "sp", "sg", "ly"):
+    for sem in ("sv", "ss", "sp", "ly") + (() if CFG["ESEND"] else ("sg",)):
         need("g", (sem, done[sem]))

@@ -24,17 +24,26 @@ CFG = {
     "HV": ("a0 a2 b0 b1 x0 z0 x1 z1 x2 z2 x3 z3 s0", "a0 a2 b0 b1 x0 y0 z0 x1 y1 z1 x2 y2 z2 x3 y3 z3 s0"),
     "HS": ("a1 a3 g0 g1 g2 b2 g3 b3", "a1 a3 g0 g1 b2 g2 b3 g3"),
 }
-CFG.update({'CUT': (256, 256, 224, 224),
+CFG.update({'CUT': (288, 288, 256, 256),
  'PICK': [[('h0', 1, ''), ('h1', 2, 'h0+h1'), ('r1', 1.5, 'r1'), ('r2', 1.5, 'r2'), ('r3', 2.0, 'r3'), ('r0', 1.5, '')],
           [('h0', 1.5, ''), ('h1', 2.0, 'h0+h1'), ('r0', 1.5, ''), ('r1', 2.0, 'r1'), ('r2', 1.5, 'r2'), ('r3', 1.5, 'r3')]],
  'ORDER': ((1, 0, 2, 3), (0, 1, 2, 3), (0, 1, 2, 3), (1, 0, 2, 3)), 'RUNS': ((), ()),
  'PE': ('0 1 23 r h', '0 1 23 r h', '0 1 2 3 r h', '0 1 2 3 r h'),
- 'HV': ('a0 a2 b0 b2 x0 x1 z0 x2 z1 x3 z2 z3 s0', 'a0 a2 b0 b1 x0 x1 y0 x2 y1 z0 x3 y2 z1 y3 z2 z3 s0'),
- 'HS': ('a1 a3 g0 b1 g1 g2 b3 g3', 'a1 a3 g0 g1 b2 g2 b3 g3'),
+ 'HP': ('a0 a1 a2 a3 b0 b1 b2 b3 p0 p1 p2 p3', 'b0 b1 b2 b3 a0 a1 a2 a3 p0 p1 p2 p3',
+        'a0 a1 a2 a3 b0 b1 b2 b3 p0 q0 p1 q1 p2 q2 p3 q3', 'a0 a1 a2 a3 b0 b1 b2 b3 p0 q0 p1 q1 p2 q2 p3 q3'),
+ 'HV': ('a0 a2 b0 b2 x0 x1 z0 x2 z1 x3 z2 z3 s0', 'b0 b2 a0 g0 a2 x0 x1 z0 x2 z1 x3 z2 z3 s0',
+        'a0 a2 b0 b1 x0 x1 y0 x2 y1 z0 x3 y2 z1 y3 z2 z3 s0', 'a0 a2 b0 b1 x0 x1 y0 x2 y1 z0 x3 y2 z1 y3 z2 z3 s0'),
+ 'HS': ('a1 a3 g0 g1 b1 g2 g3 b3', 'b1 b3 a1 g1 a3 g2 g3', 'a1 a3 g0 g1 b2 g2 b3 g3', 'a1 a3 g0 g1 b2 g2 b3 g3'),
  'WLOAD': 2,
- 'WHOLE': 'q01 p01',
+ 'WHOLE': 'relay', 'RSTEP': 1,
  'LATE': ((0, 2, 3, 4), (0, 2, 3)),
- 'FIRST': ('mwfh', 'mwa')})
+ 'FIRST': ('mwhf', 'mwa')})
+_X0, _X1 = ' x0 x1 z00 x2 z10 x3 z20 z30 s0 z01 z11 z21 z31 s1', ' x0 x1 y0 x2 y1 z00 x3 y2 z10 y3 z20 z30 s0 z01 z11 z21 z31 s1'
+CFG.update(HV=("a0 a2 b0 b2" + _X0, "b0 b2 a0 g0 a2" + _X0, "a0 a2 b0 b1" + _X1, "a0 a2 b0 b1" + _X1), RUNS=((160,), (128,)),
+ PICK=[[('h0', 1, ''), ('h1', 2, 'h0+h1'), ('r1', 1.5, 'r1'), ('r2', 1.5, 'r2'), ('r3', 2.0, 'r3'), ('r0', 1.5, '')],
+       [('h0', 1.5, ''), ('h1', 2, 'h0+h1'), ('r1', 2.0, 'r1'), ('r0', 1.0, ''), ('r2', 2, 'r2'), ('r3', 1.0, 'r3')]],
+ PE=('0 1 2 3 h r i', '0 1 23 h r i', '0 1 23 h r i', '0 1 23 h r i'), LATE=(("h0", "r1", "r2"), ("h0", "r1", "r0", "r2")),
+ WLOAD="r1", ESTEP=1, HSTEP=1, EARLY=96, BOTH=())
 
 SCRATCH = {
     "ids8": ("sbuf", [128, 32], "int32"),
@@ -75,7 +84,7 @@ for _s in range(4):
 for _b in range(8):
     SCRATCH["ps%d" % _b] = ("psum", [128, 512], "float32")
 
-SEMAPHORES = ["sv", "ss", "sp", "sg", "li", "lt", "lw", "ly", "sent", "lh", "av0", "av1", "ae"] + \
+SEMAPHORES = ["sv", "ss", "sp", "sg", "li", "lt", "lw", "ly", "sent", "lh", "av0", "av1", "ae", "aq", "ap"] + \
     ["la%d" % x for x in range(1, 4)] + ["ar%d" % x for x in range(4)]
 
 
@@ -127,6 +136,9 @@ def rank_program(g, core, T, topo):
             m = fin("sv", V.quantize_mx(T.eq[:, 128 * b:128 * b + 128], T.ep[:, 128 * b:128 * b + 128], T.e[:, 4 - b:516 - b]))
         return m
 
+    def per(key, q):
+        return CFG[key][q if len(CFG[key]) == 4 else q // 2]
+
     def runs(q):
         cuts = (0,) + CFG["RUNS"][q // 2] + (CUT[q],)
         return list(zip(cuts, cuts[1:]))
@@ -152,7 +164,7 @@ def rank_program(g, core, T, topo):
         return n
 
     def landed(q, name):
-        for _, _, calls in CFG["PICK"][q // 2]:
+        for _, _, calls in per("PICK", q):
             for call in calls.split():
                 parts = call.split("+")
                 if name in parts:
@@ -169,35 +181,49 @@ def rank_program(g, core, T, topo):
         m_e = constants()
         if CFG["ESEND"]:
             need("g", m_e)
-            send([(T.cores[r], u8(T.eq, 0, 512), u8(T.eq, 0, 512), "ae")], step=CFG["HSTEP"])
-            send([(T.cores[r], T.ep[:], T.ep[:], "ae")], step=CFG["HSTEP"])
-        xa, xb = ((2 ^ r, 3 ^ r), (0 ^ r, 1 ^ r))[kind]
+            send([(T.cores[r], u8(T.eq, 0, 512), u8(T.eq, 0, 512), "ae")], step=CFG["ESTEP"])
+            send([(T.cores[r], T.ep[:], T.ep[:], "ae")], step=CFG["ESTEP"])
+        xa, xb = ((2 ^ r, 3 ^ r), (2, 3))[kind]
         xp, xq = ((0, 1), (2 ^ r, 3 ^ r))[kind]
         m_off = ("lh", len(addr_engines(r)[3]))
         m_pick = {x: landed(r ^ x, "h%d" % x) for x in (0, 1)}
         mk = {}
-        todo = {"p": CFG["HP"][kind].split(), "v": CFG["HV"][kind].split(), "s": CFG["HS"][kind].split()}
+        todo = {q: CFG["H" + q.upper()][r if len(CFG["H" + q.upper()]) == 4 else kind].split() for q in "pvs"}
+        if CFG["WHOLE"] == "relay":
+            both = CFG.get("BOTH", ())
+            direct = len(share(T.cores[r ^ 2], core, 0, 1 + (r ^ 2 in both)))
+            m_whole = {2: [("aq", direct), ("ap", direct)], 3: [("ar3", 2 * len(share(helper[r ^ 1], core, 0, 1, CFG["RSTEP"])))]}
+            if r ^ 3 in both:
+                m_whole[3] = [("ar3", 2 * len(share(T.cores[r ^ 3], core, 1, 2)))]
+            if r ^ 2 not in both:
+                need("g", m_whole[2][0])
+                send([(helper[r ^ 1], u8(T.rq2, 0, K), u8(T.rq3, 0, K), "ar3")], step=CFG["RSTEP"])
+                need("g", m_whole[2][1])
+                send([(helper[r ^ 1], T.rp2[:], T.rp3[:], "ar3")], step=CFG["RSTEP"])
+        else:
+            m_whole = {x: [("ar%d" % x, whole_engines(r ^ x, r))] for x in (2, 3)}
+        bank = {"a": 4 * (xa - 2), "b": 4 * (xb - 2), "p": 0, "q": 4}
 
         def step(q, op):
             c, b = op[0], int(op[1])
             if q == "p":
                 if c in "ab":
-                    x = 2 + (c == "b")
-                    need("p", m_e, ("ar%d" % x, whole_engines(r ^ (xa if c == "a" else xb), r)))
-                    mk["d" + c, b] = decode(4 * (c == "b"), T["rq%d" % x], T["rp%d" % x], 0, K, True, True, (b,))[0]
+                    x = xa if c == "a" else xb
+                    need("p", m_e, *m_whole[x])
+                    mk["d" + c, b] = decode(bank[c], T["rq%d" % x], T["rp%d" % x], 0, K, True, True, (b,))[0]
                 else:
-                    free = ("a" if c == "p" else "b", b)
+                    free = ("a" if bank[c] == bank["a"] else "b", b)
                     if free not in mk:
                         return False
                     xs = (xp, xq) if kind == 0 else (xp if c == "p" else xq,)
                     for x in xs:
                         need("p", mk[free], m_pick[x])
-                        mk["d" + c, b] = decode(4 * (c == "q"), T["rq%d" % x], T["rp%d" % x], 0, n, x == xs[0], x == xs[-1], (b,))[0]
+                        mk["d" + c, b] = decode(bank[c], T["rq%d" % x], T["rp%d" % x], 0, n, x == xs[0], x == xs[-1], (b,))[0]
             elif c in "ab":
                 if ("d" + c, b) not in mk:
                     return False
                 need(q, mk["d" + c, b])
-                mk[c, b] = copy(q, T["d" + c][:, K * b:K * b + K], T["ps%d" % (4 * (c == "b") + b)][:])
+                mk[c, b] = copy(q, T["d" + c][:, K * b:K * b + K], T["ps%d" % (bank[c] + b)][:])
             elif c == "g":
                 if ("a", b) not in mk:
                     return False
@@ -227,7 +253,7 @@ def rank_program(g, core, T, topo):
                 mk[c, b] = fin("sv", V.tensor_tensor(T.vt[:, 4 * lo + b:4 * hi:4] if c == "z" else acc, new, old, ADD))
             return True
 
-        while any(todo.values()):
+        for _ in range(40):
             for q in "pvs":
                 while todo[q] and step(q, todo[q][0]):
                     todo[q].pop(0)
@@ -245,7 +271,7 @@ def rank_program(g, core, T, topo):
         j = i + 4
         m_ids = fin("li", S.dma_start(T.ids8[16 * j:16 * j + 16, :], T.ids[:, :]), 16)
     m_tb = fin("lt", Y.dma_start(T.tbt[:], T.tb[:, :]), 16)
-    m_e = ("ae", 2 * len(share(helper[r], core, 0, 1, CFG["HSTEP"]))) if CFG["ESEND"] else constants()
+    m_e = ("ae", 2 * len(share(helper[r], core, 0, 1, CFG["ESTEP"]))) if CFG["ESEND"] else constants()
 
     tabs = [r ^ 1, r, r ^ 2, r ^ 3]
 
@@ -279,13 +305,17 @@ def rank_program(g, core, T, topo):
             send([(T.cores[r ^ 1], T.near[:, 0, :], T.even[:, 0, :], "la1")], ae[0:1])
         elif op == "w":
             need("g", m_tq)
-            x = 2 + r % 2
+            if CFG["WHOLE"] == "relay":
+                m = 1 + (r in CFG.get("BOTH", ()))
+                send([(helper[r ^ 2], u8(T.tq, 0, K), u8(T.rq2, 0, K), "aq"), (helper[r ^ 3], u8(T.tq, 0, K), u8(T.rq3, 0, K), "ar3")][:m])
+                send([(helper[r ^ 2], T.tp[:], T.rp2[:], "ap"), (helper[r ^ 3], T.tp[:], T.rp3[:], "ar3")][:m])
+                return
             for call in CFG["WHOLE"].split():
-                src, dst = (u8(T.tq, 0, K), u8(T["rq%d" % x], 0, K)) if call[0] == "q" else (T.tp[:], T["rp%d" % x][:])
-                if len(call) == 1:
-                    send([([helper[r ^ 2], helper[r ^ 3]], src, dst, "ar%d" % x)])
+                xs = [2 + int(i) for i in call[1:]]
+                if call[0] == "q":
+                    send([(helper[r ^ x], u8(T.tq, 0, K), u8(T["rq%d" % x], 0, K), "ar%d" % x) for x in xs])
                 else:
-                    send([(helper[r ^ (2 + int(i))], src, dst, "ar%d" % x) for i in call[1:]])
+                    send([(helper[r ^ x], T.tp[:], T["rp%d" % x][:], "ar%d" % x) for x in xs])
         else:
             need("g", m_far)
             items = [(T.cores[r ^ x], T.far[:, x - 2, 0:2 * kr], T.even[:, x - 1, 0:2 * kr], "la%d" % x) for x in (2, 3)]
@@ -331,10 +361,10 @@ def rank_program(g, core, T, topo):
 
     def part(name):
         x = int(name[1])
-        return (x,) + {"h": (0, CUT[r ^ x]), "r": (CUT[r ^ x], TOK), "a": (0, TOK)}[name[0]]
+        return (x,) + {"h": (0, CUT[r ^ x]), "r": (CUT[r ^ x], TOK), "a": (0, TOK), "e": (n, n + CFG["EARLY"])}[name[0]]
 
-    stages = CFG["PICK"][r // 2]
-    late, mk = [], {}
+    stages = per("PICK", r)
+    late, mk, early = [], {}, []
 
     def pack_w():
         need("v", mk["w"])
@@ -344,7 +374,7 @@ def rank_program(g, core, T, topo):
         name, _, calls = stages[i]
         x, a, z = part(name)
         m = pack(x, a, z, marks)
-        if i == CFG["WLOAD"]:
+        if name == CFG["WLOAD"]:
             need("y", m)
             mk["w"] = fin("lw", Y.dma_start(T.wt[:], T.w[:, :]), 16)
         if x == 0 and z == TOK:
@@ -362,10 +392,13 @@ def rank_program(g, core, T, topo):
         if x > 1 and (x, 1) not in m_off:
             w2 = (TOK - CUT[r ^ 2]) // 8
             m_off[2, 1] = m_off[3, 1] = plus1(T.odd[:, 1:3, 0:w2], T.even[:, 1:3, 0:w2], m_la[2], m_la[3])
-        marks = gather(x, a, z, nv)
+        if name == "e0":
+            early = gather(x, a, z, nv)
+            continue
+        marks = early + gather(x, a + CFG["EARLY"], z, nv) if name == "r0" and early else gather(x, a, z, nv)
         if i == len(stages) - 1 and not calls:
             pack_w()
-        if i in CFG["LATE"][r // 2]:
+        if name in per("LATE", r):
             late.append(lambda i=i, marks=marks: close(i, marks))
         else:
             close(i, marks)

@@ -5,56 +5,38 @@ N, TOK, K, O = 4, 512, 512, 2
 HA = (1237, 1811, 947, 1543)
 HB = (40503, 12289, 58111, 3571)
 COPY = ActivationFunctionType.Copy
-ADD = AluOpType.add
+ADD, MULT = AluOpType.add, AluOpType.mult
+SHIFT, AND = AluOpType.logical_shift_right, AluOpType.bitwise_and
+_AB, _BA = "a0 a1 a2 a3 b0 b1 b2 b3 ", "b0 b1 b2 b3 a0 a1 a2 a3 "
+_P, _PQ = "p0 p1 p2 p3", "p0 q0 p1 q1 p2 q2 p3 q3"
+_XZ = " x0 x1 z00 x2 z10 x3 z20 z30 s0 Z01 Z11 Z21 Z31 s1"
+_XYZ = " x0 x1 y00 x2 y10 z00 x3 y20 z10 y30 z20 z30 y01 s0 y11 y21 y31 z01 z11 z21 z31 s1"
 CFG = {
-    "CUT": (256, 256, 192, 192),
-    "WLOAD": 1,
-    "PICK": [[("h0", 1, ""), ("h1", 2, "h0+h1"), ("r2", 2, "r2"), ("r3", 1, "r3"), ("r1", 2, "r1"), ("r0", 1, "")]] * 2,
-    "ORDER": ((0, 1, 2, 3), (1, 0, 2, 3), (0, 1, 2, 3), (1, 0, 2, 3)),
-    "PE": ("0123 r h", "0123 r h", "0 1 23 r h", "0 1 23 r h"),
-    "STEP": 1,
-    "HSTEP": 2,
-    "ESEND": 1,
-    "AE": ((0, 4), (4, 6), (6, 8), (8, 10)),
-    "FIRST": ("mwfh", "mwa"),
-    "LATE": ((0, 2, 3), (0, 2, 3)),
-    "WHOLE": "q01 p01",
-    "RUNS": ((), ()),
-    "HP": ("a0 a1 a2 a3 b0 b1 b2 b3 p0 p1 p2 p3", "a0 a1 a2 a3 b0 b1 b2 b3 p0 q0 p1 q1 p2 q2 p3 q3"),
-    "HV": ("a0 a2 b0 b1 x0 z0 x1 z1 x2 z2 x3 z3 s0", "a0 a2 b0 b1 x0 y0 z0 x1 y1 z1 x2 y2 z2 x3 y3 z3 s0"),
-    "HS": ("a1 a3 g0 g1 g2 b2 g3 b3", "a1 a3 g0 g1 b2 g2 b3 g3"),
+    "CUT": (256, 256, 256, 256),
+    "RUNS": ((128,), (128,)),
+    "PICK": [[("h0", 1, ""), ("h1", 2, "h0+h1"), ("r1", 1.5, "r1"), ("r2", 1.5, "r2"), ("a3", 2, "a3"), ("b3", 2, "b3"), ("a0", 1, ""), ("b0", 1, "")],
+             [("h0", 1, ""), ("h1", 2, "h0+h1"), ("r1", 1.5, "r1"), ("r2", 1.5, "r2"), ("r3", 2, "r3"), ("r0", 1.5, "")]],
+    "LATE": (("h0", "r1", "r2", "a3", "b3"), ("h0", "r1", "r2")),
+    "WLOAD": "r1",
+    "ORDER": ((1, 0, 2, 3), (0, 1, 2, 3), (0, 1, 2, 3), (1, 0, 2, 3)),
+    "PE": ("0 0s 12 3 123s r h s i",) + ("0 0s 1 23 123s r h s i",) * 3,
+    "LIST": 8,
+    "HP": (_AB + _P, _BA + _P, _AB + _PQ, _AB + _PQ),
+    "HV": ("a0 a2 b0 b2" + _XZ, "b0 b2 a0 g0 a2" + _XZ, "a0 a2 b0 b1" + _XYZ, "a0 a2 b0 b1" + _XYZ),
+    "HS": ("a1 a3 g0 g1 b1 g2 g3 b3 G01 G11 G21 G31", "b1 b3 a1 g1 a3 g2 g3 G01 G11 G21 G31", "a1 a3 g0 g1 b2 g2 b3 g3", "a1 a3 g0 g1 b2 g2 b3 g3"),
 }
-CFG.update({'CUT': (288, 288, 256, 256),
- 'PICK': [[('h0', 1, ''), ('h1', 2, 'h0+h1'), ('r1', 1.5, 'r1'), ('r2', 1.5, 'r2'), ('r3', 2.0, 'r3'), ('r0', 1.5, '')],
-          [('h0', 1.5, ''), ('h1', 2.0, 'h0+h1'), ('r0', 1.5, ''), ('r1', 2.0, 'r1'), ('r2', 1.5, 'r2'), ('r3', 1.5, 'r3')]],
- 'ORDER': ((1, 0, 2, 3), (0, 1, 2, 3), (0, 1, 2, 3), (1, 0, 2, 3)), 'RUNS': ((), ()),
- 'PE': ('0 1 23 r h', '0 1 23 r h', '0 1 2 3 r h', '0 1 2 3 r h'),
- 'HP': ('a0 a1 a2 a3 b0 b1 b2 b3 p0 p1 p2 p3', 'b0 b1 b2 b3 a0 a1 a2 a3 p0 p1 p2 p3',
-        'a0 a1 a2 a3 b0 b1 b2 b3 p0 q0 p1 q1 p2 q2 p3 q3', 'a0 a1 a2 a3 b0 b1 b2 b3 p0 q0 p1 q1 p2 q2 p3 q3'),
- 'HV': ('a0 a2 b0 b2 x0 x1 z0 x2 z1 x3 z2 z3 s0', 'b0 b2 a0 g0 a2 x0 x1 z0 x2 z1 x3 z2 z3 s0',
-        'a0 a2 b0 b1 x0 x1 y0 x2 y1 z0 x3 y2 z1 y3 z2 z3 s0', 'a0 a2 b0 b1 x0 x1 y0 x2 y1 z0 x3 y2 z1 y3 z2 z3 s0'),
- 'HS': ('a1 a3 g0 g1 b1 g2 g3 b3', 'b1 b3 a1 g1 a3 g2 g3', 'a1 a3 g0 g1 b2 g2 b3 g3', 'a1 a3 g0 g1 b2 g2 b3 g3'),
- 'WLOAD': 2,
- 'WHOLE': 'relay', 'RSTEP': 1,
- 'LATE': ((0, 2, 3, 4), (0, 2, 3)),
- 'FIRST': ('mwhf', 'mwa')})
-_X0, _X1 = ' x0 x1 z00 x2 z10 x3 z20 z30 s0 z01 z11 z21 z31 s1', ' x0 x1 y0 x2 y1 z00 x3 y2 z10 y3 z20 z30 s0 z01 z11 z21 z31 s1'
-CFG.update(HV=("a0 a2 b0 b2" + _X0, "b0 b2 a0 g0 a2" + _X0, "a0 a2 b0 b1" + _X1, "a0 a2 b0 b1" + _X1), RUNS=((160,), (128,)),
- PICK=[[('h0', 1, ''), ('h1', 2, 'h0+h1'), ('r1', 1.5, 'r1'), ('r2', 1.5, 'r2'), ('r3', 2.0, 'r3'), ('r0', 1.5, '')],
-       [('h0', 1.5, ''), ('h1', 2, 'h0+h1'), ('r1', 2.0, 'r1'), ('r0', 1.0, ''), ('r2', 2, 'r2'), ('r3', 1.0, 'r3')]],
- PE=('0 1 2 3 h r i', '0 1 23 h r i', '0 1 23 h r i', '0 1 23 h r i'), LATE=(("h0", "r1", "r2"), ("h0", "r1", "r0", "r2")),
- WLOAD="r1", ESTEP=1, HSTEP=1, EARLY=96, BOTH=())
 
 SCRATCH = {
     "ids8": ("sbuf", [128, 32], "int32"),
-    "hx": ("sbuf", [128, 128], "int32"),
+    "idsm": ("sbuf", [128, 32], "int32"),
+    "hx": ("sbuf", [128, 4, 32], "int32"),
     "hh": ("sbuf", [128, 4, 32], "int32"),
-    "near": ("sbuf", [128, 2, 64], "uint16"),
-    "nearo": ("sbuf", [128, 64], "uint16"),
+    "off0": ("sbuf", [128, 4, 32], "uint16"),
+    "off1": ("sbuf", [128, 4, 32], "uint16"),
     "far": ("sbuf", [128, 2, 64], "uint16"),
+    "even": ("sbuf", [128, 2, 64], "uint16"),
+    "odd": ("sbuf", [128, 2, 64], "uint16"),
     "hlp": ("sbuf", [128, 64], "uint16"),
-    "even": ("sbuf", [128, 3, 64], "uint16"),
-    "odd": ("sbuf", [128, 3, 64], "uint16"),
     "hoff": ("sbuf", [128, 64], "uint16"),
     "tbt": ("sbuf", [128, 4 * K], "bfloat16"),
     "tq": ("sbuf", [128, K], "float8_e4m3fn_x4"),
@@ -69,6 +51,7 @@ SCRATCH = {
     "da": ("sbuf", [128, 4 * K], "bfloat16"),
     "db": ("sbuf", [128, 4 * K], "bfloat16"),
     "ga": ("sbuf", [128, 4 * TOK], "bfloat16"),
+    "gb": ("sbuf", [128, 4 * TOK], "bfloat16"),
     "acc": ("sbuf", [128, 4 * TOK], "float32"),
     "vt": ("sbuf", [128, 4 * TOK], "bfloat16"),
     "vq": ("sbuf", [128, TOK], "float8_e4m3fn_x4"),
@@ -84,8 +67,8 @@ for _s in range(4):
 for _b in range(8):
     SCRATCH["ps%d" % _b] = ("psum", [128, 512], "float32")
 
-SEMAPHORES = ["sv", "ss", "sp", "sg", "li", "lt", "lw", "ly", "sent", "lh", "av0", "av1", "ae", "aq", "ap"] + \
-    ["la%d" % x for x in range(1, 4)] + ["ar%d" % x for x in range(4)]
+SEMAPHORES = ["sv", "ss", "sp", "sg", "li", "lt", "lw", "ly", "sent", "av0", "av1", "ae", "aq", "ap"] + \
+    ["la%d" % x for x in range(1, 4)] + ["ar%d" % x for x in range(4)] + ["br%d" % x for x in range(1, 4)]
 
 
 def rank_program(g, core, T, topo):
@@ -97,6 +80,8 @@ def rank_program(g, core, T, topo):
     Q = {"v": V, "s": S, "p": P, "g": g, "y": Y}
     CUT = CFG["CUT"]
     done, seen, local = {}, {}, [0]
+    engines = topo.engines(T.cores[0], T.cores[1])
+    E = len(engines)
 
     def fin(sem, ins, n=1):
         ins.then_inc(T.sem[sem], n)
@@ -109,100 +94,70 @@ def rank_program(g, core, T, topo):
                 Q[q].wait_ge(T.sem[sem], n)
                 seen[(q, sem)] = n
 
-    def share(src, dst, i, n, step=None):
-        es = topo.engines(src, dst)[::step or CFG["STEP"]]
-        e = len(es)
-        cut = {1: (0, e), 2: (0, e // 2, e), 3: (0, e // 4, e // 2, e)}[n]
-        return es[cut[i]:cut[i + 1]]
-
-    def send(items, es=None, step=None):
-        tr = []
-        for i, (dst_core, src, dst, sem) in enumerate(items):
-            cores = dst_core if isinstance(dst_core, list) else [dst_core]
-            e = es[i] if es else share(core, cores[0], i, len(items), step)
+    def send(items, e=E):
+        tr, e = [], e // len(items)
+        for i, (cores, src, dst, sem) in enumerate(items):
             tr.append(RemoteDMATransfer(dst_ids=[DstId(rid=topo.addr(c)[0], pnc=topo.addr(c)[1]) for c in cores],
-                                        dma_engine_mask=sum(1 << k for k in e), remote_sem=T.sem[sem], srcs=[src], dsts=[dst] * len(cores)))
-            local[0] += len(e)
+                                        dma_engine_mask=sum(1 << k for k in engines[e * i:e * i + e]),
+                                        remote_sem=T.sem[sem], srcs=[src], dsts=[dst] * len(cores)))
+            local[0] += e
         g.remote_dma_fused(tr, local_sem=T.sem.sent)
 
     def u8(buf, a, z):
         return buf[:, a:z].bitcast(dt.uint8)
 
-    def constants():
-        m_eye = fin("sg", g.iota(T.eye[:], [[-1, 128]], 0, 1, allow_small_or_imprecise_dtypes=True))
-        need("v", fin("sv", V.memset(T.e[:], 0.0)), m_eye)
-        need("v", fin("sv", V.tensor_scalar(T.e[:, 4:516:4], T.eye[:], 0.0, None, AluOpType.is_equal)))
-        for b in range(4):
-            m = fin("sv", V.quantize_mx(T.eq[:, 128 * b:128 * b + 128], T.ep[:, 128 * b:128 * b + 128], T.e[:, 4 - b:516 - b]))
-        return m
-
     def per(key, q):
         return CFG[key][q if len(CFG[key]) == 4 else q // 2]
 
     def runs(q):
-        cuts = (0,) + CFG["RUNS"][q // 2] + (CUT[q],)
+        cuts = (0,) + per("RUNS", q) + (CUT[q],)
         return list(zip(cuts, cuts[1:]))
 
-    def decode(base, cq, cp, a, z, start, stop, banks):
-        ms = []
-        for b in banks:
-            ms.append(fin("sp", P.matmul_mx(T["ps%d" % (base + b)][:, 0:z - a], T.eq[:, 128 * b:128 * b + 128],
-                                            T.ep[:, 128 * b:128 * b + 128], cq[:, a:z], cp[:, a:z], start, stop)))
-        return ms
+    def decode(bank, b, cq, cp, a, z, start, stop):
+        return fin("sp", P.matmul_mx(T["ps%d" % bank][:, 0:z - a], T.eq[:, 128 * b:128 * b + 128], T.ep[:, 128 * b:128 * b + 128],
+                                     cq[:, a:z], cp[:, a:z], start, stop))
 
     def copy(q, out, src):
         return fin("sv", V.tensor_copy(out, src)) if q == "v" else fin("ss", S.activation(out, src, COPY))
 
-    def whole_engines(q, h):
-        n = 0
-        for call in CFG["WHOLE"].split():
-            i = str((h ^ q) % 2)
-            if len(call) == 1:
-                n += len(share(T.cores[q], helper[h], 0, 1))
-            elif i in call:
-                n += len(share(T.cores[q], helper[h], call.index(i) - 1, len(call) - 1))
-        return n
+    def ts(out, src, *args):
+        return fin("sv", V.tensor_scalar(out, src, *args))
+
+    def sem_of(name):
+        return ("br" if name[0] == "b" else "ar") + name[1]
 
     def landed(q, name):
         for _, _, calls in per("PICK", q):
             for call in calls.split():
-                parts = call.split("+")
-                if name in parts:
-                    return ("ar" + name[1], 2 * len(share(T.cores[q], core, parts.index(name), len(parts))))
+                if name in call.split("+"):
+                    return (sem_of(name), 2 * (E // len(call.split("+"))))
 
-    def addr_engines(q):
-        es = topo.engines(T.cores[q], T.cores[q ^ 1])[::CFG["STEP"]]
-        return [es[a:z] for a, z in CFG["AE"]]
+    m_list = ("la1", CFG["LIST"])
+    FE = E // 4
 
     if core in helper:
         r = helper.index(core)
         n, kind = CUT[r], r // 2
         k = n // 16
-        m_e = constants()
-        if CFG["ESEND"]:
-            need("g", m_e)
-            send([(T.cores[r], u8(T.eq, 0, 512), u8(T.eq, 0, 512), "ae")], step=CFG["ESTEP"])
-            send([(T.cores[r], T.ep[:], T.ep[:], "ae")], step=CFG["ESTEP"])
+        m_eye = fin("sg", g.iota(T.eye[:], [[-1, 128]], 0, 1, allow_small_or_imprecise_dtypes=True))
+        need("v", fin("sv", V.memset(T.e[:], 0.0)), m_eye)
+        need("v", ts(T.e[:, 4:516:4], T.eye[:], 0.0, None, AluOpType.is_equal))
+        for b in range(4):
+            m_e = fin("sv", V.quantize_mx(T.eq[:, 128 * b:128 * b + 128], T.ep[:, 128 * b:128 * b + 128], T.e[:, 4 - b:516 - b]))
+        need("g", m_e)
+        send([([T.cores[r]], u8(T.eq, 0, 512), u8(T.eq, 0, 512), "ae")])
+        send([([T.cores[r]], T.ep[:], T.ep[:], "ae")])
+        m_off = ("la1", FE)
+        m_whole = {2: [("aq", E), ("ap", E)], 3: [("ar3", 2 * E)]}
+        need("g", m_whole[2][0])
+        send([([helper[r ^ 1]], u8(T.rq2, 0, K), u8(T.rq3, 0, K), "ar3")])
+        need("g", m_whole[2][1])
+        send([([helper[r ^ 1]], T.rp2[:], T.rp3[:], "ar3")])
         xa, xb = ((2 ^ r, 3 ^ r), (2, 3))[kind]
         xp, xq = ((0, 1), (2 ^ r, 3 ^ r))[kind]
-        m_off = ("lh", len(addr_engines(r)[3]))
-        m_pick = {x: landed(r ^ x, "h%d" % x) for x in (0, 1)}
-        mk = {}
-        todo = {q: CFG["H" + q.upper()][r if len(CFG["H" + q.upper()]) == 4 else kind].split() for q in "pvs"}
-        if CFG["WHOLE"] == "relay":
-            both = CFG.get("BOTH", ())
-            direct = len(share(T.cores[r ^ 2], core, 0, 1 + (r ^ 2 in both)))
-            m_whole = {2: [("aq", direct), ("ap", direct)], 3: [("ar3", 2 * len(share(helper[r ^ 1], core, 0, 1, CFG["RSTEP"])))]}
-            if r ^ 3 in both:
-                m_whole[3] = [("ar3", 2 * len(share(T.cores[r ^ 3], core, 1, 2)))]
-            if r ^ 2 not in both:
-                need("g", m_whole[2][0])
-                send([(helper[r ^ 1], u8(T.rq2, 0, K), u8(T.rq3, 0, K), "ar3")], step=CFG["RSTEP"])
-                need("g", m_whole[2][1])
-                send([(helper[r ^ 1], T.rp2[:], T.rp3[:], "ar3")], step=CFG["RSTEP"])
-        else:
-            m_whole = {x: [("ar%d" % x, whole_engines(r ^ x, r))] for x in (2, 3)}
         bank = {"a": 4 * (xa - 2), "b": 4 * (xb - 2), "p": 0, "q": 4}
+        mk = {}
+        todo = {q: CFG["H" + q.upper()][r].split() for q in "pvs"}
 
         def step(q, op):
             c, b = op[0], int(op[1])
@@ -210,47 +165,57 @@ def rank_program(g, core, T, topo):
                 if c in "ab":
                     x = xa if c == "a" else xb
                     need("p", m_e, *m_whole[x])
-                    mk["d" + c, b] = decode(bank[c], T["rq%d" % x], T["rp%d" % x], 0, K, True, True, (b,))[0]
+                    mk["d" + c, b] = decode(bank[c] + b, b, T["rq%d" % x], T["rp%d" % x], 0, K, True, True)
                 else:
                     free = ("a" if bank[c] == bank["a"] else "b", b)
                     if free not in mk:
                         return False
                     xs = (xp, xq) if kind == 0 else (xp if c == "p" else xq,)
                     for x in xs:
-                        need("p", mk[free], m_pick[x])
-                        mk["d" + c, b] = decode(bank[c], T["rq%d" % x], T["rp%d" % x], 0, n, x == xs[0], x == xs[-1], (b,))[0]
+                        need("p", mk[free], landed(r ^ x, "h%d" % x))
+                        mk["d" + c, b] = decode(bank[c] + b, b, T["rq%d" % x], T["rp%d" % x], 0, n, x == xs[0], x == xs[-1])
             elif c in "ab":
                 if ("d" + c, b) not in mk:
                     return False
                 need(q, mk["d" + c, b])
                 mk[c, b] = copy(q, T["d" + c][:, K * b:K * b + K], T["ps%d" % (bank[c] + b)][:])
-            elif c == "g":
-                if ("a", b) not in mk:
+            elif c in "gG":
+                src, x = ("a", xa) if c == "g" else ("b", xb)
+                if (src, b) not in mk:
                     return False
-                need(q, mk["a", b], m_off)
-                mk[c, b] = copy(q, T.ga[:, n * b:n * b + n], T.da[:, K * b:K * b + K].indirect(T.hoff[:, (xa - 2) * k:(xa - 1) * k]))
+                lo, hi = runs(r)[int(op[2])] if op[2:] else (0, n)
+                need(q, mk[src, b], m_off)
+                m = copy(q, T["g" + src][:, n * b + lo:n * b + hi],
+                         T["d" + src][:, K * b:K * b + K].indirect(T.hoff[:, (x - 2) * k + lo // 16:(x - 2) * k + hi // 16]))
+                for u in op[2:] or "01":
+                    mk[c, b, u] = m
             elif c == "s":
                 lo, hi = runs(r)[b]
-                need("v", *[mk["z", i] for i in range(4)])
+                need("v", *[mk["z", i, str(b)] for i in range(4)])
                 need("g", fin("sv", V.quantize_mx(T.vq[:, lo:hi], T.vp[:, lo:hi], T.vt[:, 4 * lo:4 * hi])))
-                send([(T.cores[r], u8(T.vq, lo, hi), u8(T.vq, lo, hi), "av%d" % b)], step=CFG["HSTEP"])
-                send([(T.cores[r], T.vp[:, lo:hi], T.vp[:, lo:hi], "av%d" % b)], step=CFG["HSTEP"])
+                send([([T.cores[r]], u8(T.vq, lo, hi), u8(T.vq, lo, hi), "av%d" % b)])
+                send([([T.cores[r]], T.vp[:, lo:hi], T.vp[:, lo:hi], "av%d" % b)])
             else:
                 lo, hi = runs(r)[int(op[2])] if op[2:] else (0, n)
-                before = {"x": "g", "y": "x", "z": "xy"[kind]}[c]
+                ready, c = c.isupper(), c.lower()
+                before = [({"x": "g", "y": "x", "z": "xy"[kind]}[c], b, u) for u in op[2:] or "01"]
                 picked = (c == "z") if kind == 0 else (c == "x")
-                src = ("b" if picked else "dq" if c == "z" else "dp", b)
-                if (before, b) not in mk or src not in mk:
+                src = ("G", b, op[2]) if ready else ("b" if picked else "dq" if c == "z" else "dp", b)
+                if any(u not in mk for u in before + [src]):
                     return False
                 acc = T.acc[:, n * b + lo:n * b + hi]
                 old = T.ga[:, n * b + lo:n * b + hi] if c == "x" else acc
-                need("v", mk[src], mk[before, b])
-                if picked:
+                need("v", mk[src], *[mk[u] for u in before])
+                if ready:
+                    new = T.gb[:, n * b + lo:n * b + hi]
+                elif picked:
                     need("v", m_off)
                     new = T.db[:, K * b:K * b + K].indirect(T.hoff[:, (xb - 2) * k + lo // 16:(xb - 2) * k + hi // 16])
                 else:
-                    new = T["ps%d" % (4 * (src[0] == "dq") + b)][:, lo:hi]
-                mk[c, b] = fin("sv", V.tensor_tensor(T.vt[:, 4 * lo + b:4 * hi:4] if c == "z" else acc, new, old, ADD))
+                    new = T["ps%d" % (bank[src[0][1]] + b)][:, lo:hi]
+                m = fin("sv", V.tensor_tensor(T.vt[:, 4 * lo + b:4 * hi:4] if c == "z" else acc, new, old, ADD))
+                for u in op[2:] or "01":
+                    mk[c, b, u] = m
             return True
 
         for _ in range(40):
@@ -271,166 +236,144 @@ def rank_program(g, core, T, topo):
         j = i + 4
         m_ids = fin("li", S.dma_start(T.ids8[16 * j:16 * j + 16, :], T.ids[:, :]), 16)
     m_tb = fin("lt", Y.dma_start(T.tbt[:], T.tb[:, :]), 16)
-    m_e = ("ae", 2 * len(share(helper[r], core, 0, 1, CFG["ESTEP"]))) if CFG["ESEND"] else constants()
+    m_e = ("ae", 2 * E)
+    need("g", m_ids)
+    send([([T.cores[r ^ 1]], T.ids8[:], T.idsm[:], "la1")], CFG["LIST"])
 
-    tabs = [r ^ 1, r, r ^ 2, r ^ 3]
-
-    def plus1(out, src, *marks):
-        need("v", *marks)
-        return fin("sv", V.tensor_scalar(out, src, 1, None, ADD))
-
-    ae = addr_engines(r)
+    m_off = {}
     need("v", m_ids)
-    m_hx = [fin("sv", V.tensor_scalar(T.hx[:, 32 * s:32 * s + 32], T.ids8[:], HA[tabs[s]], HB[tabs[s]], AluOpType.mult, ADD)) for s in range(4)]
-    m_hh = []
-    for s in (0, 2):
-        need("v", m_hx[s + 1])
-        m_hh.append(fin("sv", V.tensor_scalar(T.hh[:, s:s + 2, :], T.hx[:, 32 * s:32 * s + 64], 3, 4 * (K - 1),
-                                              AluOpType.logical_shift_right, AluOpType.bitwise_and)))
-    need("v", m_hh[0])
-    fin("sv", V.tensor_copy(T.near[:, :, 0:32], T.hh[:, 0:2, :]))
-    m_ev = fin("sv", V.tensor_scalar(T.near[:, :, 32:64], T.hh[:, 0:2, :], 2, None, ADD))
-    need("v", m_hh[1])
-    fin("sv", V.tensor_copy(T.far[:, :, 0:kr], T.hh[:, 2:4, k:32]))
-    m_od = plus1(T.nearo[:], T.near[:, 1, :], m_ev)
-    fin("sv", V.tensor_scalar(T.far[:, :, kr:2 * kr], T.hh[:, 2:4, k:32], 2, None, ADD))
-    m_far = fin("sv", V.tensor_scalar(T.hlp[:, 0:2 * k], T.hh[:, 2:4, 0:k], 0.25, None, AluOpType.mult))
-    m_la = {x: ("la%d" % x, len(ae[x - 1])) for x in (1, 2, 3)}
+    m_hx = [ts(T.hx[:, x, :], T.ids8[:], HA[r ^ x], HB[r ^ x], MULT, ADD) for x in (0, 2, 3)]
+    need("v", m_hx[0])
+    m_own = ts(T.hh[:, 0, :], T.hx[:, 0, :], 3, 4 * (K - 1), SHIFT, AND)
+    need("v", m_hx[2])
+    m_hf = ts(T.hh[:, 2:4, :], T.hx[:, 2:4, :], 3, 4 * (K - 1), SHIFT, AND)
+    need("v", m_own)
+    for t in (2, 0, 3, 1):
+        m_off[0, t] = ts(T.off0[:, t, :], T.hh[:, 0, :], t, None, ADD)
+
     need("v", m_tb)
-    m_tq = fin("sv", V.quantize_mx(T.tq[:], T.tp[:], T.tbt[:]))
+    need("g", fin("sv", V.quantize_mx(T.tq[:], T.tp[:], T.tbt[:])))
+    send([([helper[r ^ 2]], u8(T.tq, 0, K), u8(T.rq2, 0, K), "aq")])
+    send([([helper[r ^ 2]], T.tp[:], T.rp2[:], "ap")])
 
-    def first_calls(op):
-        if op == "m":
-            need("g", m_ev)
-            send([(T.cores[r ^ 1], T.near[:, 0, :], T.even[:, 0, :], "la1")], ae[0:1])
-        elif op == "w":
-            need("g", m_tq)
-            if CFG["WHOLE"] == "relay":
-                m = 1 + (r in CFG.get("BOTH", ()))
-                send([(helper[r ^ 2], u8(T.tq, 0, K), u8(T.rq2, 0, K), "aq"), (helper[r ^ 3], u8(T.tq, 0, K), u8(T.rq3, 0, K), "ar3")][:m])
-                send([(helper[r ^ 2], T.tp[:], T.rp2[:], "ap"), (helper[r ^ 3], T.tp[:], T.rp3[:], "ar3")][:m])
-                return
-            for call in CFG["WHOLE"].split():
-                xs = [2 + int(i) for i in call[1:]]
-                if call[0] == "q":
-                    send([(helper[r ^ x], u8(T.tq, 0, K), u8(T["rq%d" % x], 0, K), "ar%d" % x) for x in xs])
-                else:
-                    send([(helper[r ^ x], T.tp[:], T["rp%d" % x][:], "ar%d" % x) for x in xs])
-        else:
-            need("g", m_far)
-            items = [(T.cores[r ^ x], T.far[:, x - 2, 0:2 * kr], T.even[:, x - 1, 0:2 * kr], "la%d" % x) for x in (2, 3)]
-            items.append((helper[r], T.hlp[:, 0:2 * k], T.hoff[:, 0:2 * k], "lh"))
-            if op == "a":
-                send(items, ae[1:])
-            elif op == "f":
-                send(items[0:2], ae[1:3])
+    def mate(i):
+        if i == 0:
+            need("v", m_list)
+            mk["m"] = ts(T.hx[:, 1, :], T.idsm[:], HA[r], HB[r], MULT, ADD)
+            need("v", m_hf)
+            ts(T.far[:, :, 0:kr], T.hh[:, 2:4, k:32], 0, None, ADD)
+            ts(T.hlp[:, 0:2 * k], T.hh[:, 2:4, 0:k], 0.25, None, MULT)
+        elif i == 1:
+            need("v", mk["m"])
+            mk["m"] = ts(T.hh[:, 1, :], T.hx[:, 1, :], 3, 4 * (K - 1), SHIFT, AND)
+            need("g", ts(T.far[:, :, kr:2 * kr], T.hh[:, 2:4, k:32], 2, None, ADD))
+            items = [([helper[r]], T.hlp[:, 0:2 * k], T.hoff[:, 0:2 * k], "la1")]
+            items += [([T.cores[r ^ x]], T.far[:, x - 2, 0:2 * kr], T.even[:, x - 2, 0:2 * kr], "la%d" % x) for x in (2, 3)]
+            if k == kr:
+                send(items, 3 * FE)
             else:
-                send(items[2:], ae[3:])
-
-    for op in CFG["FIRST"][k == kr]:
-        first_calls(op)
-
-    m_off = {(0, 0): m_ev, (0, 1): m_od}
-    for x in (1, 2, 3):
-        m_off[x, 0] = m_la[x]
+                send(items[:1], FE)
+                send(items[1:], 2 * FE)
+        else:
+            need("v", mk["m"])
+            for t in (2, 0, 3, 1):
+                m_off[1, t] = ts(T.off1[:, t, :], T.hh[:, 1, :], t, None, ADD)
 
     def gather(x, a, z, nv):
         marks = []
         for t in (0, 2, 1, 3):
-            first = 32 * (t // 2) if x < 2 else (z - a) // 16 * (t // 2) - a // 16
             mid = a + round(min(1, max(0, nv - t)) * (z - a) / 32) * 32
             for q, lo, hi in (("v", a, mid), ("s", mid, z)):
                 if lo == hi:
                     continue
-                cols = slice(first + lo // 16, first + hi // 16)
-                if x == 0:
-                    off = T.nearo[:, cols] if t % 2 else T.near[:, 1, cols]
+                if x < 2:
+                    off = T["off%d" % x][:, t, lo // 16:hi // 16]
                 else:
-                    off = (T.odd if t % 2 else T.even)[:, x - 1, cols]
-                need(q, m_tb, m_off[x, t % 2])
+                    first = (TOK - CUT[r ^ x]) // 16 * (t // 2) - CUT[r ^ x] // 16
+                    off = (T.odd if t % 2 else T.even)[:, x - 2, first + lo // 16:first + hi // 16]
+                need(q, m_tb, m_off[x, t])
                 marks.append(copy(q, T["gt%d" % x][:, 4 * lo + t:4 * hi:4], T.tbt[:].indirect(off)))
                 if q == "v" and late:
-                    late.pop()()
-        if late:
-            late.pop()()
+                    late.pop(0)()
+        while late:
+            late.pop(0)()
         return marks
-
-    def pack(x, a, z, marks):
-        need("v", *marks)
-        return fin("sv", V.quantize_mx(T["gq%d" % x][:, a:z], T["gp%d" % x][:, a:z], T["gt%d" % x][:, 4 * a:4 * z]))
 
     def part(name):
         x = int(name[1])
-        return (x,) + {"h": (0, CUT[r ^ x]), "r": (CUT[r ^ x], TOK), "a": (0, TOK), "e": (n, n + CFG["EARLY"])}[name[0]]
+        return (x,) + {"h": (0, CUT[r ^ x]), "r": (CUT[r ^ x], TOK), "a": (CUT[r ^ x], TOK - 128), "b": (TOK - 128, TOK)}[name[0]]
 
     stages = per("PICK", r)
-    late, mk, early = [], {}, []
+    late, mk = [], {}
 
     def pack_w():
         need("v", mk["w"])
         mk["wq"] = fin("sv", V.quantize_mx(T.wq[:], T.wp[:], T.wt[:]))
 
-    def close(i, marks):
-        name, _, calls = stages[i]
+    def close(name, calls, marks):
         x, a, z = part(name)
-        m = pack(x, a, z, marks)
+        need("v", *marks)
+        mk[name] = fin("sv", V.quantize_mx(T["gq%d" % x][:, a:z], T["gp%d" % x][:, a:z], T["gt%d" % x][:, 4 * a:4 * z]))
         if name == CFG["WLOAD"]:
-            need("y", m)
+            need("y", mk[name])
             mk["w"] = fin("lw", Y.dma_start(T.wt[:], T.w[:, :]), 16)
-        if x == 0 and z == TOK:
-            mk["own"] = m
         for call in calls.split():
-            need("g", m)
-            parts = [((helper if u[0] == "h" else T.cores)[r ^ int(u[1])],) + part(u) for u in call.split("+")]
-            send([(c, u8(T["gq%d" % x], a, z), u8(T["rq%d" % x], a, z), "ar%d" % x) for c, x, a, z in parts])
-            send([(c, T["gp%d" % x][:, a:z], T["rp%d" % x][:, a:z], "ar%d" % x) for c, x, a, z in parts])
+            need("g", mk[name])
+            parts = [([(helper if u[0] == "h" else T.cores)[r ^ int(u[1])]], sem_of(u)) + part(u) for u in call.split("+")]
+            send([(c, u8(T["gq%d" % x], a, z), u8(T["rq%d" % x], a, z), sem) for c, sem, x, a, z in parts])
+            send([(c, T["gp%d" % x][:, a:z], T["rp%d" % x][:, a:z], sem) for c, sem, x, a, z in parts])
 
-    for i, (name, nv, calls) in enumerate(stages):
+    for name, nv, calls in stages:
         x, a, z = part(name)
-        if x == 1 and (x, 1) not in m_off:
-            m_off[x, 1] = plus1(T.odd[:, 0, :], T.even[:, 0, :], m_la[1])
-        if x > 1 and (x, 1) not in m_off:
+        if name == "h0":
+            late += [lambda i=i: mate(i) for i in range(3)]
+        if x > 1 and (x, 0) not in m_off:
             w2 = (TOK - CUT[r ^ 2]) // 8
-            m_off[2, 1] = m_off[3, 1] = plus1(T.odd[:, 1:3, 0:w2], T.even[:, 1:3, 0:w2], m_la[2], m_la[3])
-        if name == "e0":
-            early = gather(x, a, z, nv)
-            continue
-        marks = early + gather(x, a + CFG["EARLY"], z, nv) if name == "r0" and early else gather(x, a, z, nv)
-        if i == len(stages) - 1 and not calls:
-            pack_w()
+            need("v", ("la2", FE), ("la3", FE))
+            m = ts(T.odd[:, :, 0:w2], T.even[:, :, 0:w2], 1, None, ADD)
+            for u in (2, 3):
+                m_off[u, 0] = m_off[u, 2] = ("la%d" % u, FE)
+                m_off[u, 1] = m_off[u, 3] = m
+        marks = gather(x, a, z, nv)
         if name in per("LATE", r):
-            late.append(lambda i=i, marks=marks: close(i, marks))
+            late.append(lambda name=name, calls=calls, marks=marks: close(name, calls, marks))
         else:
-            close(i, marks)
-    if calls:
-        pack_w()
-    m_own, m_wq = mk["own"], mk["wq"]
+            close(name, calls, marks)
+    pack_w()
 
     order = CFG["ORDER"][r]
-    m_vq = {"hi"[i]: ("av%d" % i, 2 * len(share(helper[r], core, 0, 1, CFG["HSTEP"]))) for i in range(2)}
+    m_vq = {"h": ("av0", 2 * E), "i": ("av1", 2 * E)}
     ops = CFG["PE"][r].split()
+    split = "s" in ops
+    span = {"h": runs(r)[0], "i": runs(r)[-1], "r": (n, TOK - 128 if split else TOK), "s": (TOK - 128, TOK)}
+    banks = {"h": 0, "r": 2, "i": 4, "s": 6} if split else {"r": 4, "h": 6, "i": 0}
+    mv = {}
     for op in ops:
-        if op.isdigit():
-            sums = []
+        if op[0].isdigit():
+            run = "s" if op[-1] == "s" else "r"
+            (a, z), base = span[run], 4 * (run == "s")
+            sums = {}
             for b in range(4):
-                for i in map(int, op):
+                for i in map(int, op.strip("s")):
                     x = order[i] ^ r
-                    cq, cp, m = (T["rq%d" % x], T["rp%d" % x], landed(r ^ x, "r%d" % x)) if x else (T.gq0, T.gp0, m_own)
+                    name = "ab"[run == "s"] + str(x)
+                    if x:
+                        cq, cp, m = T["rq%d" % x], T["rp%d" % x], landed(r ^ x, "r%d" % x) or landed(r ^ x, name)
+                    else:
+                        cq, cp, m = T.gq0, T.gp0, mk.get("r0") or mk[name]
                     need("p", m_e, m)
-                    m = decode(0, cq, cp, n, TOK, i == 0, i == 3, banks=(b,))
-                sums += m
+                    sums[b] = decode(base + b, b, cq, cp, a, z, i == 0, i == 3)
             if i == 3:
-                mv = []
                 for b in range(4):
                     need("vs"[b % 2], sums[b])
-                    mv.append(copy("vs"[b % 2], T.vt[:, 4 * n + b:4 * TOK:4], T["ps%d" % b][:, 0:TOK - n]))
-                need("v", *mv)
-                m_vq["r"] = fin("sv", V.quantize_mx(T.vq[:, n:TOK], T.vp[:, n:TOK], T.vt[:, 4 * n:4 * TOK]))
+                    mv[base + b] = copy("vs"[b % 2], T.vt[:, 4 * a + b:4 * z:4], T["ps%d" % (base + b)][:, 0:z - a])
+                need("v", *[mv[base + b] for b in range(4)])
+                m_vq[run] = fin("sv", V.quantize_mx(T.vq[:, a:z], T.vp[:, a:z], T.vt[:, 4 * a:4 * z]))
             continue
-        (a, z), base = ((n, TOK), 4) if op == "r" else (runs(r)[0], 6) if op == "h" else (runs(r)[1], 0)
-        need("p", m_wq, m_vq[op])
-        if op == "i":
-            need("p", *mv)
+        (a, z), base = span[op], banks[op]
+        need("p", mk["wq"], m_vq[op])
+        if split or op == "i":
+            need("p", mv[base], mv[base + 1])
         my = [fin("sp", P.matmul_mx(T["ps%d" % (base + o)][:, 0:z - a], T.wq[:, 128 * o:128 * o + 128], T.wp[:, 128 * o:128 * o + 128],
                                     T.vq[:, a:z], T.vp[:, a:z], True, True)) for o in range(O)]
         for o in range(O):
@@ -441,5 +384,5 @@ def rank_program(g, core, T, topo):
             need(dq, m)
             fin("ly", Q[dq].dma_start(T.y[:, lo:lo + z - a], T.yt[:, lo:lo + z - a]), 16)
     g.wait_ge(T.sem.sent, local[0])
-    for sem in ("sv", "ss", "sp", "ly") + (() if CFG["ESEND"] else ("sg",)):
+    for sem in ("sv", "ss", "sp", "ly"):
         need("g", (sem, done[sem]))

from concourse.bass import DstId, RemoteDMATransfer
from concourse.mybir import dt, AluOpType, ActivationFunctionType

N, TOK, K, O = 4, 512, 512, 2
HA = (1237, 1811, 947, 1543)
HB = (40503, 12289, 58111, 3571)
COPY = ActivationFunctionType.Copy
ADD, MULT = AluOpType.add, AluOpType.mult
SHIFT, AND = AluOpType.logical_shift_right, AluOpType.bitwise_and
_AB, _BA = "a0 a1 a2 a3 b0 b1 b2 b3 ", "b0 b1 b2 b3 a0 a1 a2 a3 "
_P, _PQ = "p0 p1 p2 p3", "p0 q0 p1 q1 p2 q2 p3 q3"
_XZ = " x0 x1 z00 x2 z10 x3 z20 z30 s0 Z01 Z11 Z21 Z31 s1"
_XYZ = " x0 x1 y00 x2 y10 z00 x3 y20 z10 y30 z20 z30 y01 s0 y11 y21 y31 z01 z11 z21 z31 s1"
CFG = {
    "CUT": (256, 256, 256, 256),
    "RUNS": ((128,), (128,)),
    "PICK": [[("h0", 1, ""), ("h1", 2, "h0+h1"), ("r1", 1.5, "r1"), ("r2", 1.5, "r2"), ("a3", 2, "a3"), ("b3", 2, "b3"), ("a0", 1, ""), ("b0", 1, "")],
             [("h0", 1, ""), ("h1", 2, "h0+h1"), ("r1", 1.5, "r1"), ("r2", 1.5, "r2"), ("r3", 2, "r3"), ("r0", 1.5, "")]],
    "LATE": (("h0", "r1", "r2", "a3", "b3"), ("h0", "r1", "r2")),
    "WLOAD": "r1",
    "ORDER": ((1, 0, 2, 3), (0, 1, 2, 3), (0, 1, 2, 3), (1, 0, 2, 3)),
    "PE": ("0 0s 12 3 123s r h s i",) + ("0 0s 1 23 123s r h s i",) * 3,
    "LIST": 8,
    "HP": (_AB + _P, _BA + _P, _AB + _PQ, _AB + _PQ),
    "HV": ("a0 a2 b0 b2" + _XZ, "b0 b2 a0 g0 a2" + _XZ, "a0 a2 b0 b1" + _XYZ, "a0 a2 b0 b1" + _XYZ),
    "HS": ("a1 a3 g0 g1 b1 g2 g3 b3 G01 G11 G21 G31", "b1 b3 a1 g1 a3 g2 g3 G01 G11 G21 G31", "a1 a3 g0 g1 b2 g2 b3 g3", "a1 a3 g0 g1 b2 g2 b3 g3"),
}

SCRATCH = {
    "ids8": ("sbuf", [128, 32], "int32"),
    "idsm": ("sbuf", [128, 32], "int32"),
    "hx": ("sbuf", [128, 4, 32], "int32"),
    "hh": ("sbuf", [128, 4, 32], "int32"),
    "off0": ("sbuf", [128, 4, 32], "uint16"),
    "off1": ("sbuf", [128, 4, 32], "uint16"),
    "far": ("sbuf", [128, 2, 64], "uint16"),
    "even": ("sbuf", [128, 2, 64], "uint16"),
    "odd": ("sbuf", [128, 2, 64], "uint16"),
    "hlp": ("sbuf", [128, 64], "uint16"),
    "hoff": ("sbuf", [128, 64], "uint16"),
    "tbt": ("sbuf", [128, 4 * K], "bfloat16"),
    "tq": ("sbuf", [128, K], "float8_e4m3fn_x4"),
    "tp": ("sbuf", [128, K], "uint8"),
    "wt": ("sbuf", [128, 512 * O], "bfloat16"),
    "wq": ("sbuf", [128, 128 * O], "float8_e4m3fn_x4"),
    "wp": ("sbuf", [128, 128 * O], "uint8"),
    "eye": ("sbuf", [128, 128], "bfloat16"),
    "e": ("sbuf", [128, 528], "bfloat16"),
    "eq": ("sbuf", [128, 512], "float8_e4m3fn_x4"),
    "ep": ("sbuf", [128, 512], "uint8"),
    "da": ("sbuf", [128, 4 * K], "bfloat16"),
    "db": ("sbuf", [128, 4 * K], "bfloat16"),
    "ga": ("sbuf", [128, 4 * TOK], "bfloat16"),
    "gb": ("sbuf", [128, 4 * TOK], "bfloat16"),
    "acc": ("sbuf", [128, 4 * TOK], "float32"),
    "vt": ("sbuf", [128, 4 * TOK], "bfloat16"),
    "vq": ("sbuf", [128, TOK], "float8_e4m3fn_x4"),
    "vp": ("sbuf", [128, TOK], "uint8"),
    "yt": ("sbuf", [128, O * TOK], "float32"),
}
for _s in range(4):
    SCRATCH["gt%d" % _s] = ("sbuf", [128, 4 * TOK], "bfloat16")
    SCRATCH["gq%d" % _s] = ("sbuf", [128, TOK], "float8_e4m3fn_x4")
    SCRATCH["gp%d" % _s] = ("sbuf", [128, TOK], "uint8")
    SCRATCH["rq%d" % _s] = ("sbuf", [128, TOK], "float8_e4m3fn_x4")
    SCRATCH["rp%d" % _s] = ("sbuf", [128, TOK], "uint8")
for _b in range(8):
    SCRATCH["ps%d" % _b] = ("psum", [128, 512], "float32")

SEMAPHORES = ["sv", "ss", "sp", "sg", "li", "lt", "lw", "ly", "sent", "av0", "av1", "ae", "aq", "ap"] + \
    ["la%d" % x for x in range(1, 4)] + ["ar%d" % x for x in range(4)] + ["br%d" % x for x in range(1, 4)]


def rank_program(g, core, T, topo):
    spare = [c for c in topo.cores_of(T.cores[0]) if c not in T.cores]
    helper = [[c for c in spare if topo.die(c) == topo.die(T.cores[q ^ 2])][q % 2] for q in range(N)]
    if core not in T.cores and core not in helper:
        return
    V, S, P, Y = g.vector, g.scalar, g.tensor, g.sync
    Q = {"v": V, "s": S, "p": P, "g": g, "y": Y}
    CUT = CFG["CUT"]
    done, seen, local = {}, {}, [0]
    engines = topo.engines(T.cores[0], T.cores[1])
    E = len(engines)

    def fin(sem, ins, n=1):
        ins.then_inc(T.sem[sem], n)
        done[sem] = done.get(sem, 0) + n
        return (sem, done[sem])

    def need(q, *marks):
        for sem, n in marks:
            if seen.get((q, sem), 0) < n:
                Q[q].wait_ge(T.sem[sem], n)
                seen[(q, sem)] = n

    def send(items, e=E):
        tr, e = [], e // len(items)
        for i, (cores, src, dst, sem) in enumerate(items):
            tr.append(RemoteDMATransfer(dst_ids=[DstId(rid=topo.addr(c)[0], pnc=topo.addr(c)[1]) for c in cores],
                                        dma_engine_mask=sum(1 << k for k in engines[e * i:e * i + e]),
                                        remote_sem=T.sem[sem], srcs=[src], dsts=[dst] * len(cores)))
            local[0] += e
        g.remote_dma_fused(tr, local_sem=T.sem.sent)

    def u8(buf, a, z):
        return buf[:, a:z].bitcast(dt.uint8)

    def per(key, q):
        return CFG[key][q if len(CFG[key]) == 4 else q // 2]

    def runs(q):
        cuts = (0,) + per("RUNS", q) + (CUT[q],)
        return list(zip(cuts, cuts[1:]))

    def decode(bank, b, cq, cp, a, z, start, stop):
        return fin("sp", P.matmul_mx(T["ps%d" % bank][:, 0:z - a], T.eq[:, 128 * b:128 * b + 128], T.ep[:, 128 * b:128 * b + 128],
                                     cq[:, a:z], cp[:, a:z], start, stop))

    def copy(q, out, src):
        return fin("sv", V.tensor_copy(out, src)) if q == "v" else fin("ss", S.activation(out, src, COPY))

    def ts(out, src, *args):
        return fin("sv", V.tensor_scalar(out, src, *args))

    def sem_of(name):
        return ("br" if name[0] == "b" else "ar") + name[1]

    def landed(q, name):
        for _, _, calls in per("PICK", q):
            for call in calls.split():
                if name in call.split("+"):
                    return (sem_of(name), 2 * (E // len(call.split("+"))))

    m_list = ("la1", CFG["LIST"])
    FE = E // 4

    if core in helper:
        r = helper.index(core)
        n, kind = CUT[r], r // 2
        k = n // 16
        m_eye = fin("sg", g.iota(T.eye[:], [[-1, 128]], 0, 1, allow_small_or_imprecise_dtypes=True))
        need("v", fin("sv", V.memset(T.e[:], 0.0)), m_eye)
        need("v", ts(T.e[:, 4:516:4], T.eye[:], 0.0, None, AluOpType.is_equal))
        for b in range(4):
            m_e = fin("sv", V.quantize_mx(T.eq[:, 128 * b:128 * b + 128], T.ep[:, 128 * b:128 * b + 128], T.e[:, 4 - b:516 - b]))
        need("g", m_e)
        send([([T.cores[r]], u8(T.eq, 0, 512), u8(T.eq, 0, 512), "ae")])
        send([([T.cores[r]], T.ep[:], T.ep[:], "ae")])
        m_off = ("la1", FE)
        m_whole = {2: [("aq", E), ("ap", E)], 3: [("ar3", 2 * E)]}
        need("g", m_whole[2][0])
        send([([helper[r ^ 1]], u8(T.rq2, 0, K), u8(T.rq3, 0, K), "ar3")])
        need("g", m_whole[2][1])
        send([([helper[r ^ 1]], T.rp2[:], T.rp3[:], "ar3")])
        xa, xb = ((2 ^ r, 3 ^ r), (2, 3))[kind]
        xp, xq = ((0, 1), (2 ^ r, 3 ^ r))[kind]
        bank = {"a": 4 * (xa - 2), "b": 4 * (xb - 2), "p": 0, "q": 4}
        mk = {}
        todo = {q: CFG["H" + q.upper()][r].split() for q in "pvs"}

        def step(q, op):
            c, b = op[0], int(op[1])
            if q == "p":
                if c in "ab":
                    x = xa if c == "a" else xb
                    need("p", m_e, *m_whole[x])
                    mk["d" + c, b] = decode(bank[c] + b, b, T["rq%d" % x], T["rp%d" % x], 0, K, True, True)
                else:
                    free = ("a" if bank[c] == bank["a"] else "b", b)
                    if free not in mk:
                        return False
                    xs = (xp, xq) if kind == 0 else (xp if c == "p" else xq,)
                    for x in xs:
                        need("p", mk[free], landed(r ^ x, "h%d" % x))
                        mk["d" + c, b] = decode(bank[c] + b, b, T["rq%d" % x], T["rp%d" % x], 0, n, x == xs[0], x == xs[-1])
            elif c in "ab":
                if ("d" + c, b) not in mk:
                    return False
                need(q, mk["d" + c, b])
                mk[c, b] = copy(q, T["d" + c][:, K * b:K * b + K], T["ps%d" % (bank[c] + b)][:])
            elif c in "gG":
                src, x = ("a", xa) if c == "g" else ("b", xb)
                if (src, b) not in mk:
                    return False
                lo, hi = runs(r)[int(op[2])] if op[2:] else (0, n)
                need(q, mk[src, b], m_off)
                m = copy(q, T["g" + src][:, n * b + lo:n * b + hi],
                         T["d" + src][:, K * b:K * b + K].indirect(T.hoff[:, (x - 2) * k + lo // 16:(x - 2) * k + hi // 16]))
                for u in op[2:] or "01":
                    mk[c, b, u] = m
            elif c == "s":
                lo, hi = runs(r)[b]
                need("v", *[mk["z", i, str(b)] for i in range(4)])
                need("g", fin("sv", V.quantize_mx(T.vq[:, lo:hi], T.vp[:, lo:hi], T.vt[:, 4 * lo:4 * hi])))
                send([([T.cores[r]], u8(T.vq, lo, hi), u8(T.vq, lo, hi), "av%d" % b)])
                send([([T.cores[r]], T.vp[:, lo:hi], T.vp[:, lo:hi], "av%d" % b)])
            else:
                lo, hi = runs(r)[int(op[2])] if op[2:] else (0, n)
                ready, c = c.isupper(), c.lower()
                before = [({"x": "g", "y": "x", "z": "xy"[kind]}[c], b, u) for u in op[2:] or "01"]
                picked = (c == "z") if kind == 0 else (c == "x")
                src = ("G", b, op[2]) if ready else ("b" if picked else "dq" if c == "z" else "dp", b)
                if any(u not in mk for u in before + [src]):
                    return False
                acc = T.acc[:, n * b + lo:n * b + hi]
                old = T.ga[:, n * b + lo:n * b + hi] if c == "x" else acc
                need("v", mk[src], *[mk[u] for u in before])
                if ready:
                    new = T.gb[:, n * b + lo:n * b + hi]
                elif picked:
                    need("v", m_off)
                    new = T.db[:, K * b:K * b + K].indirect(T.hoff[:, (xb - 2) * k + lo // 16:(xb - 2) * k + hi // 16])
                else:
                    new = T["ps%d" % (bank[src[0][1]] + b)][:, lo:hi]
                m = fin("sv", V.tensor_tensor(T.vt[:, 4 * lo + b:4 * hi:4] if c == "z" else acc, new, old, ADD))
                for u in op[2:] or "01":
                    mk[c, b, u] = m
            return True

        for _ in range(40):
            for q in "pvs":
                while todo[q] and step(q, todo[q][0]):
                    todo[q].pop(0)
        g.wait_ge(T.sem.sent, local[0])
        for sem in ("sv", "ss", "sp", "sg"):
            need("g", (sem, done[sem]))
        return

    r = T.rank_of(core)
    n = CUT[r]
    k, kr = n // 16, (TOK - n) // 16

    for i in range(4):
        fin("li", Y.dma_start(T.ids8[16 * i:16 * i + 16, :], T.ids[:, :]), 16)
        j = i + 4
        m_ids = fin("li", S.dma_start(T.ids8[16 * j:16 * j + 16, :], T.ids[:, :]), 16)
    m_tb = fin("lt", Y.dma_start(T.tbt[:], T.tb[:, :]), 16)
    m_e = ("ae", 2 * E)
    need("g", m_ids)
    send([([T.cores[r ^ 1]], T.ids8[:], T.idsm[:], "la1")], CFG["LIST"])

    m_off = {}
    need("v", m_ids)
    m_hx = [ts(T.hx[:, x, :], T.ids8[:], HA[r ^ x], HB[r ^ x], MULT, ADD) for x in (0, 2, 3)]
    need("v", m_hx[0])
    m_own = ts(T.hh[:, 0, :], T.hx[:, 0, :], 3, 4 * (K - 1), SHIFT, AND)
    need("v", m_hx[2])
    m_hf = ts(T.hh[:, 2:4, :], T.hx[:, 2:4, :], 3, 4 * (K - 1), SHIFT, AND)
    need("v", m_own)
    for t in (2, 0, 3, 1):
        m_off[0, t] = ts(T.off0[:, t, :], T.hh[:, 0, :], t, None, ADD)

    need("v", m_tb)
    need("g", fin("sv", V.quantize_mx(T.tq[:], T.tp[:], T.tbt[:])))
    send([([helper[r ^ 2]], u8(T.tq, 0, K), u8(T.rq2, 0, K), "aq")])
    send([([helper[r ^ 2]], T.tp[:], T.rp2[:], "ap")])

    def mate(i):
        if i == 0:
            need("v", m_list)
            mk["m"] = ts(T.hx[:, 1, :], T.idsm[:], HA[r], HB[r], MULT, ADD)
            need("v", m_hf)
            ts(T.far[:, :, 0:kr], T.hh[:, 2:4, k:32], 0, None, ADD)
            ts(T.hlp[:, 0:2 * k], T.hh[:, 2:4, 0:k], 0.25, None, MULT)
        elif i == 1:
            need("v", mk["m"])
            mk["m"] = ts(T.hh[:, 1, :], T.hx[:, 1, :], 3, 4 * (K - 1), SHIFT, AND)
            need("g", ts(T.far[:, :, kr:2 * kr], T.hh[:, 2:4, k:32], 2, None, ADD))
            items = [([helper[r]], T.hlp[:, 0:2 * k], T.hoff[:, 0:2 * k], "la1")]
            items += [([T.cores[r ^ x]], T.far[:, x - 2, 0:2 * kr], T.even[:, x - 2, 0:2 * kr], "la%d" % x) for x in (2, 3)]
            if k == kr:
                send(items, 3 * FE)
            else:
                send(items[:1], FE)
                send(items[1:], 2 * FE)
        else:
            need("v", mk["m"])
            for t in (2, 0, 3, 1):
                m_off[1, t] = ts(T.off1[:, t, :], T.hh[:, 1, :], t, None, ADD)

    def gather(x, a, z, nv):
        marks = []
        for t in (0, 2, 1, 3):
            mid = a + round(min(1, max(0, nv - t)) * (z - a) / 32) * 32
            for q, lo, hi in (("v", a, mid), ("s", mid, z)):
                if lo == hi:
                    continue
                if x < 2:
                    off = T["off%d" % x][:, t, lo // 16:hi // 16]
                else:
                    first = (TOK - CUT[r ^ x]) // 16 * (t // 2) - CUT[r ^ x] // 16
                    off = (T.odd if t % 2 else T.even)[:, x - 2, first + lo // 16:first + hi // 16]
                need(q, m_tb, m_off[x, t])
                marks.append(copy(q, T["gt%d" % x][:, 4 * lo + t:4 * hi:4], T.tbt[:].indirect(off)))
                if q == "v" and late:
                    late.pop(0)()
        while late:
            late.pop(0)()
        return marks

    def part(name):
        x = int(name[1])
        return (x,) + {"h": (0, CUT[r ^ x]), "r": (CUT[r ^ x], TOK), "a": (CUT[r ^ x], TOK - 128), "b": (TOK - 128, TOK)}[name[0]]

    stages = per("PICK", r)
    late, mk = [], {}

    def pack_w():
        need("v", mk["w"])
        mk["wq"] = fin("sv", V.quantize_mx(T.wq[:], T.wp[:], T.wt[:]))

    def close(name, calls, marks):
        x, a, z = part(name)
        need("v", *marks)
        mk[name] = fin("sv", V.quantize_mx(T["gq%d" % x][:, a:z], T["gp%d" % x][:, a:z], T["gt%d" % x][:, 4 * a:4 * z]))
        if name == CFG["WLOAD"]:
            need("y", mk[name])
            mk["w"] = fin("lw", Y.dma_start(T.wt[:], T.w[:, :]), 16)
        for call in calls.split():
            need("g", mk[name])
            parts = [([(helper if u[0] == "h" else T.cores)[r ^ int(u[1])]], sem_of(u)) + part(u) for u in call.split("+")]
            send([(c, u8(T["gq%d" % x], a, z), u8(T["rq%d" % x], a, z), sem) for c, sem, x, a, z in parts])
            send([(c, T["gp%d" % x][:, a:z], T["rp%d" % x][:, a:z], sem) for c, sem, x, a, z in parts])

    for name, nv, calls in stages:
        x, a, z = part(name)
        if name == "h0":
            late += [lambda i=i: mate(i) for i in range(3)]
        if x > 1 and (x, 0) not in m_off:
            w2 = (TOK - CUT[r ^ 2]) // 8
            need("v", ("la2", FE), ("la3", FE))
            m = ts(T.odd[:, :, 0:w2], T.even[:, :, 0:w2], 1, None, ADD)
            for u in (2, 3):
                m_off[u, 0] = m_off[u, 2] = ("la%d" % u, FE)
                m_off[u, 1] = m_off[u, 3] = m
        marks = gather(x, a, z, nv)
        if name in per("LATE", r):
            late.append(lambda name=name, calls=calls, marks=marks: close(name, calls, marks))
        else:
            close(name, calls, marks)
    pack_w()

    order = CFG["ORDER"][r]
    m_vq = {"h": ("av0", 2 * E), "i": ("av1", 2 * E)}
    ops = CFG["PE"][r].split()
    split = "s" in ops
    span = {"h": runs(r)[0], "i": runs(r)[-1], "r": (n, TOK - 128 if split else TOK), "s": (TOK - 128, TOK)}
    banks = {"h": 0, "r": 2, "i": 4, "s": 6} if split else {"r": 4, "h": 6, "i": 0}
    mv = {}
    for op in ops:
        if op[0].isdigit():
            run = "s" if op[-1] == "s" else "r"
            (a, z), base = span[run], 4 * (run == "s")
            sums = {}
            for b in range(4):
                for i in map(int, op.strip("s")):
                    x = order[i] ^ r
                    name = "ab"[run == "s"] + str(x)
                    if x:
                        cq, cp, m = T["rq%d" % x], T["rp%d" % x], landed(r ^ x, "r%d" % x) or landed(r ^ x, name)
                    else:
                        cq, cp, m = T.gq0, T.gp0, mk.get("r0") or mk[name]
                    need("p", m_e, m)
                    sums[b] = decode(base + b, b, cq, cp, a, z, i == 0, i == 3)
            if i == 3:
                for b in range(4):
                    need("vs"[b % 2], sums[b])
                    mv[base + b] = copy("vs"[b % 2], T.vt[:, 4 * a + b:4 * z:4], T["ps%d" % (base + b)][:, 0:z - a])
                need("v", *[mv[base + b] for b in range(4)])
                m_vq[run] = fin("sv", V.quantize_mx(T.vq[:, a:z], T.vp[:, a:z], T.vt[:, 4 * a:4 * z]))
            continue
        (a, z), base = span[op], banks[op]
        need("p", mk["wq"], m_vq[op])
        if split or op == "i":
            need("p", mv[base], mv[base + 1])
        my = [fin("sp", P.matmul_mx(T["ps%d" % (base + o)][:, 0:z - a], T.wq[:, 128 * o:128 * o + 128], T.wp[:, 128 * o:128 * o + 128],
                                    T.vq[:, a:z], T.vp[:, a:z], True, True)) for o in range(O)]
        for o in range(O):
            lo = TOK * o + a
            need("vs"[o], my[o])
            m = copy("vs"[o], T.yt[:, lo:lo + z - a], T["ps%d" % (base + o)][:, 0:z - a])
            dq = "s" if o == 1 and op == ops[-1] else "y"
            need(dq, m)
            fin("ly", Q[dq].dma_start(T.y[:, lo:lo + z - a], T.yt[:, lo:lo + z - a]), 16)
    g.wait_ge(T.sem.sent, local[0])
    for sem in ("sv", "ss", "sp", "ly"):
        need("g", (sem, done[sem]))
